import numpy as np
import ml_dtypes


def mxq(x, axis, fmt="e4m3"):
    dtype, down = {"e4m3": (ml_dtypes.float8_e4m3fn, 7), "e5m2": (ml_dtypes.float8_e5m2, 14)}[fmt]
    v = np.moveaxis(np.asarray(x, np.float32).astype(ml_dtypes.bfloat16).astype(np.float64), axis, -1)
    blocks = v.reshape(v.shape[:-1] + (-1, 32))
    amax = np.abs(blocks).max(-1, keepdims=True)
    byte = np.maximum(np.where(amax > 0, np.frexp(amax)[1] - 1 + 127, 0) - down, 1)
    scale = np.exp2(byte - 127.0)
    codes = (blocks / scale).astype(np.float32).astype(dtype).astype(np.float64)
    return np.moveaxis((codes * scale).reshape(v.shape), -1, axis)


WIDE = False


def mx_kscale(k):
    if not WIDE:
        return np.ones(k)
    levels = np.array([10, -10, 5, -5, 0])
    if k % 512:
        return np.exp2(np.random.permutation(np.resize(levels, k // 32))).repeat(32)
    a = np.empty((k // 512, 16))
    for p in range(k // 512):
        a[p, :8] = np.random.permutation(np.resize(levels, 8))
        for g in range(8):
            far = levels[np.abs(levels - a[p, g]) >= 10]
            a[p, g + 8] = far[np.random.randint(len(far))]
    return np.exp2(a.ravel()).repeat(32)


BF16 = ml_dtypes.bfloat16


def bf(x):
    return np.asarray(x, np.float32).astype(BF16)


def f64(x):
    return np.asarray(x).astype(np.float64)


T, A, B, U, R = 1024, 512, 1024, 512, 512


def draw0():
    s, t, u = mx_kscale(A), mx_kscale(B), mx_kscale(T)
    fade = np.exp(0.3 * np.random.standard_normal((T, 1)))
    position = A * np.random.uniform(-0.25, 0.25, (A, 1))
    direction = np.random.uniform(-1.0, 1.0, (1, B))
    phase = 2.0 * np.pi * position * direction
    return {"xr": bf(np.random.standard_normal((T, A)) * fade * s),
            "xi": bf(np.random.standard_normal((T, A)) * fade * s),
            "sr": bf(np.cos(phase) / np.sqrt(A) / s[:, None]),
            "si": bf(np.sin(phase) / np.sqrt(A) / s[:, None]),
            "window": bf((1 + 0.1 * np.random.standard_normal(T)) * u),
            "gain": bf((1 + 0.1 * np.random.standard_normal(B)) * t),
            "cr": bf(np.random.standard_normal((B, U)) / np.sqrt(B) / t[:, None]),
            "ci": bf(np.random.standard_normal((B, U)) / np.sqrt(B) / t[:, None]),
            "d": bf(np.random.standard_normal((R, T)) / np.sqrt(T) / u),
            "z_gain": bf((1 + 0.1 * np.random.standard_normal(T)) / u),
            "p_gain": bf((1 + 0.1 * np.random.standard_normal(B)) / t)}


def core(xr, xi, sr, si, window, gain, cr, ci, d, z_gain, p_gain):
    qxr = mxq(f64(xr), 1, "e4m3")
    qxi = mxq(f64(xi), 1, "e4m3")
    qsr = mxq(f64(sr), 0, "e4m3")
    qsi = mxq(f64(si), 0, "e4m3")
    yr = (qxr @ qsr) + (qxi @ qsi)
    yi = (qxi @ qsr) - (qxr @ qsi)
    power = yr ** 2 + yi ** 2
    level = np.mean(power, axis=1, keepdims=True)
    shape = f64(window)[:, None] * f64(gain)[None, :] / np.sqrt(level + power)
    hr = yr * shape
    hi = yi * shape
    zr = mxq(hr, 1, "e4m3") @ mxq(f64(cr), 0, "e4m3")
    zi = mxq(hi, 1, "e4m3") @ mxq(f64(ci), 0, "e4m3")
    z = (zr - zi) * f64(z_gain)[:, None]
    qd = mxq(f64(d), 1, "e4m3")
    er = (qd @ mxq(hr, 0, "e4m3")) * f64(p_gain)[None, :]
    ei = (qd @ mxq(hi, 0, "e4m3")) * f64(p_gain)[None, :]
    return z, er ** 2 + ei ** 2


def e4m3fn_bytes(y):
    return np.clip(np.asarray(y, np.float64), -448.0, 448.0).astype(np.float32).astype(ml_dtypes.float8_e4m3fn).view(np.uint8)


def e4m3fn_values(b):
    return np.asarray(b, np.uint8).view(ml_dtypes.float8_e4m3fn).astype(np.float64)


def setup_inputs():
    d = draw0()
    x0 = np.asarray(d['xr']).astype(np.float64)
    s = (np.max(np.abs(x0), axis=(0,), keepdims=True) / 448.0).astype(np.float32)
    out = {}
    for k, v in d.items():
        if k == 'xr':
            out['xr_bytes'] = e4m3fn_bytes(x0 / s.astype(np.float64))
            out['xr_scale'] = s
        else:
            out[k] = v
    return out


def reference(xr_bytes, xr_scale, xi, sr, si, window, gain, cr, ci, d, z_gain, p_gain):
    return core(e4m3fn_values(xr_bytes) * xr_scale.astype(np.float64), xi, sr, si, window, gain, cr, ci, d, z_gain, p_gain)

@@ -1,0 +1,499 @@
+from contextlib import ExitStack
+
+import concourse.mybir as mybir
+from concourse.masks import make_identity
+
+T, A, B, U, R = 1024, 512, 1024, 512, 512
+FLOPS = 2 * T * A * B * 4 + 2 * T * B * U * 2 + 2 * R * T * B * 2
+
+F32 = mybir.dt.float32
+BF16 = mybir.dt.bfloat16
+U32 = mybir.dt.uint32
+U8 = mybir.dt.uint8
+FP8 = mybir.dt.float8_e4m3fn
+FP8X4 = mybir.dt.float8_e4m3fn_x4
+ACT = mybir.ActivationFunctionType
+ALU = mybir.AluOpType
+
+P = 128
+PACK = 4
+HALF = 512
+YB = 6
+TB = 2
+
+
+def tile_limited_beam_combining_f6_kernel(
+    tc, xr_bytes, xr_scale, xi, sr, si, window, gain, cr, ci, d, z_gain, p_gain, out_0, out_1
+):
+    nc = tc.nc
+    with ExitStack() as ctx:
+        const = ctx.enter_context(tc.tile_pool(name="const", bufs=1))
+        xin = ctx.enter_context(tc.tile_pool(name="xin", bufs=2))
+        rawp = ctx.enter_context(tc.tile_pool(name="rawp", bufs=3))
+        grp = ctx.enter_context(tc.tile_pool(name="grp", bufs=6))
+        lim = ctx.enter_context(tc.tile_pool(name="lim", bufs=2))
+        keep = ctx.enter_context(tc.tile_pool(name="keep", bufs=1))
+        outp = ctx.enter_context(tc.tile_pool(name="outp", bufs=2))
+        psum = ctx.enter_context(tc.psum_pool(name="psum", bufs=1))
+        ctx.enter_context(tc.manual_schedule())
+
+        xr_view = xr_bytes.rearrange("(g p t) a -> g p t a", p=P, t=PACK)
+        xi_view = xi.rearrange("(g p t) a -> g p t a", p=P, t=PACK)
+        x_codes_in = [xin.tile([P, PACK, A], U8, name="xr_u8") for g in range(2)]
+        xi_in = [xin.tile([P, PACK, A], BF16, name="xi_in") for g in range(2)]
+        s_raw = [rawp.tile([P, PACK, B], BF16, name="raw") for ri in range(2)]
+        s_view = [src.rearrange("(p j) w -> p j w", j=PACK) for src in (sr, si)]
+        for ri in range(2):
+            nc.sync.dma_start(out=s_raw[ri][:, :, 0:HALF], in_=s_view[ri][:, :, 0:HALF])
+        nc.sync.dma_start(out=x_codes_in[0][:], in_=xr_view[0])
+        nc.sync.dma_start(out=xi_in[0][:], in_=xi_view[0])
+        scale_rows = const.tile([P, A], F32, name="scale_rows")
+        nc.gpsimd.memset(scale_rows[:], 0.0)
+        ident = const.tile([P, P], F32, name="ident")
+        make_identity(nc, ident[:])
+        ones_f = const.tile([P, P], F32, name="ones_f")
+        nc.vector.memset(ones_f[:], 1.0)
+        warm = const.tile([P, 1], F32, name="warm")
+        nc.vector.memset(warm[:], 1.0)
+        ident_b = const.tile([P, P], BF16, name="ident_b")
+        nc.vector.tensor_copy(out=ident_b[:], in_=ident[:])
+        neg_ident_b = const.tile([P, P], BF16, name="neg_ident_b")
+        nc.vector.tensor_scalar(out=neg_ident_b[:], in0=ident[:], scalar1=-1.0, scalar2=None, op0=ALU.mult)
+        nc.scalar.dma_start(out=scale_rows[0:1, :], in_=xr_scale)
+        for ri in range(2):
+            nc.sync.dma_start(out=s_raw[ri][:, :, HALF:B], in_=s_view[ri][:, :, HALF:B])
+        gain_bc = const.tile([P, B], BF16, name="gain_bc")
+        nc.sync.dma_start(out=gain_bc[:], in_=gain.partition_broadcast(P))
+        window_bf = const.tile([P, 2, PACK], BF16, name="window_bf")
+        nc.scalar.dma_start(out=window_bf[:], in_=window.rearrange("(g p t) -> p g t", p=P, t=PACK))
+        z_gain_bf = const.tile([P, 2, PACK], BF16, name="z_gain_bf")
+        nc.scalar.dma_start(out=z_gain_bf[:], in_=z_gain.rearrange("(g p t) -> p g t", p=P, t=PACK))
+        warm_out = const.tile([P, 1], F32, name="warm_out")
+        nc.scalar.activation(out=warm_out[:], in_=warm[:], func=ACT.Abs_reciprocal_sqrt)
+
+        nc.sync.dma_start(out=x_codes_in[1][:], in_=xr_view[1])
+        nc.sync.dma_start(out=xi_in[1][:], in_=xi_view[1])
+        c_raw = []
+        for src in (cr, ci):
+            raw = rawp.tile([P, 2, PACK, U], BF16, name="raw")
+            nc.sync.dma_start(out=raw[:], in_=src.rearrange("(g p j) v -> p g j v", p=P, j=PACK))
+            c_raw.append(raw)
+        d_raw = rawp.tile([P, 4, T], BF16, name="raw")
+        nc.sync.dma_start(out=d_raw[:], in_=d.rearrange("(q p) i -> p q i", p=P))
+
+        window_cols = const.tile([P, 2, PACK], F32, name="window_cols")
+        z_gain_cols = const.tile([P, 2, PACK], F32, name="z_gain_cols")
+        scale_bc = const.tile([P, A], F32, name="scale_bc")
+        p_gain_bc = const.tile([P, B], BF16, name="p_gain_bc")
+        nc.sync.dma_start(out=p_gain_bc[:], in_=p_gain.partition_broadcast(P))
+        pg2_bc = const.tile([P, B], F32, name="pg2_bc")
+        nc.gpsimd.tensor_tensor(out=pg2_bc[:], in0=p_gain_bc[:], in1=p_gain_bc[:], op=ALU.mult)
+
+        def broadcast(lhsT, row, out, func):
+            bank = psum.tile([P, HALF], F32, name="bank", tag="tr", bufs=TB)
+            nc.tensor.matmul(bank[:], lhsT=lhsT, rhs=row, start=True, stop=True)
+            nc.scalar.activation(out=out, in_=bank[:], func=func)
+
+        x_q = {}
+        xrb = {}
+        gx = {}
+
+        def x_product(g, ts):
+            if ts[0] == 0:
+                xrb[g] = xin.tile([P, PACK, A], BF16, name="xrb")
+            for t in ts:
+                nc.vector.tensor_tensor(
+                    out=xrb[g][:, t, :], in0=x_codes_in[g][:, t, :].bitcast(FP8), in1=scale_bc[:], op=ALU.mult
+                )
+
+        def x_turn(g, ri, pair):
+            src = (xrb, xi_in)[ri][g]
+            if pair == 0:
+                gx[(g, ri)] = grp.tile([P, 2048], BF16, name="grouped", align_bytes=64)
+            bank = psum.tile([P, 4, P], F32, name="bank", tag="tr", bufs=TB)
+            for tt in range(2):
+                words = src[:, 2 * pair + tt, :].bitcast(F32)
+                for u in range(2):
+                    nc.tensor.transpose(bank[:, 2 * tt + u, :], words[:, u : A // 2 : 2], ident[:])
+            nc.scalar.copy(
+                out=gx[(g, ri)][:, 1024 * pair : 1024 * (pair + 1)].bitcast(F32).rearrange("p (k i u) -> p k i u", k=2, u=2),
+                in_=bank[:].rearrange("p (k u) i -> p k i u", u=2),
+            )
+
+        def x_quant(g, ri):
+            codes = keep.tile([P, 512], U32, name="xq%d%d" % (g, ri), align_bytes=64)
+            scales = keep.tile([P, 512], U8, name="xs%d%d" % (g, ri), align_bytes=64)
+            nc.vector.quantize_mx(out=codes[:].bitcast(FP8X4), scales=scales[:], in_=gx[(g, ri)][:])
+            for t in range(PACK):
+                cs = slice(128 * t, 128 * t + 128)
+                x_q[(g, t, ri)] = (codes[:, cs].bitcast(FP8X4), scales[:, cs])
+
+        def interleave(engine, dst, src):
+            o = dst.rearrange("p (c i t) -> p c t i", i=4, t=PACK)
+            s = src.rearrange("p t (c i) -> p c t i", i=4)
+            if engine == "v":
+                nc.vector.tensor_copy(out=o, in_=s)
+            else:
+                nc.scalar.copy(out=o, in_=s)
+
+        def pe_group(dst, src, sign):
+            ident_pm = ident_b if sign > 0 else neg_ident_b
+            banks = []
+            for k in range(2):
+                bank = psum.tile([P, 1024], BF16, name="bank", tag="tr", bufs=TB)
+                for m in range(2):
+                    lo = 256 * k + 128 * m
+                    nc.tensor.matmul(
+                        bank[:, 512 * m : 512 * (m + 1)].rearrange("p (c t) -> p c t", t=PACK),
+                        lhsT=ident_pm[:],
+                        rhs=src[:, :, lo : lo + 128].rearrange("p t c -> p c t"),
+                        start=True,
+                        stop=True,
+                    )
+                nc.scalar.copy(out=dst[:, 1024 * k : 1024 * (k + 1)], in_=bank[:])
+
+        s_codes = [keep.tile([P, B], U32, name="s_codes%d" % k, align_bytes=64) for k in range(3)]
+        s_scales = [keep.tile([P, B], U8, name="s_scales%d" % k, align_bytes=64) for k in range(3)]
+        sg = {}
+
+        def s_group(ri, h, engine):
+            sg[(ri, h)] = grp.tile([P, 2048], BF16, name="grouped", align_bytes=64)
+            src = s_raw[ri][:, :, HALF * h : HALF * (h + 1)]
+            if engine == "t":
+                pe_group(sg[(ri, h)][:], src, 1)
+            else:
+                interleave(engine, sg[(ri, h)][:], src)
+
+        def s_neg(h):
+            sg[(2, h)] = grp.tile([P, 2048], BF16, name="grouped", align_bytes=64)
+            nc.vector.tensor_scalar(out=sg[(2, h)][:], in0=sg[(1, h)][:], scalar1=-1.0, scalar2=None, op0=ALU.mult)
+
+        def s_quant(k, h):
+            cs = slice(HALF * h, HALF * (h + 1))
+            nc.vector.quantize_mx(out=s_codes[k][:, cs].bitcast(FP8X4), scales=s_scales[k][:, cs], in_=sg[(k, h)][:])
+
+        def s_op(k, h):
+            cs = slice(HALF * h, HALF * (h + 1))
+            return s_codes[k][:, cs].bitcast(FP8X4), s_scales[k][:, cs]
+
+        def mx(out, lhs, rhs, start, stop):
+            nc.tensor.matmul_mx(
+                out=out, lhsT=lhs[0], lhsT_scale=lhs[1], rhs=rhs[0], rhs_scale=rhs[1], start=start, stop=stop
+            )
+
+        h_bf = [[keep.tile([P, PACK, B], BF16, name="h%d%d" % (g, ri)) for ri in range(2)] for g in range(2)]
+        y = {}
+        sq = {}
+        level = {}
+        power = {}
+
+        def Y(n, h):
+            g, t = divmod(n, PACK)
+            xr_op, xi_op = x_q[(g, t, 0)], x_q[(g, t, 1)]
+            yr = psum.tile([P, HALF], F32, name="y", tag="y", bufs=YB)
+            mx(yr[:], xr_op, s_op(0, h), True, False)
+            mx(yr[:], xi_op, s_op(1, h), False, True)
+            yi = psum.tile([P, HALF], F32, name="y", tag="y", bufs=YB)
+            mx(yi[:], xi_op, s_op(0, h), True, False)
+            mx(yi[:], xr_op, s_op(2, h), False, True)
+            y[(n, 0, h)], y[(n, 1, h)] = yr, yi
+
+        def SQ(n, h):
+            if h == 0:
+                sq[n] = lim.tile([P, 2, B], F32, name="sq")
+            cs = slice(HALF * h, HALF * (h + 1))
+            for ri in range(2):
+                nc.scalar.activation(out=sq[n][:, ri, cs], in_=y[(n, ri, h)][:], func=ACT.Square, scale=1.0 / 32.0)
+
+        def C(n):
+            level[n] = lim.tile([P, 1], F32, name="level")
+            power[n] = lim.tile([P, B], F32, name="power")
+            nc.vector.scalar_tensor_tensor(
+                out=power[n][:], in0=sq[n][:, 0, :], scalar=1.0, in1=sq[n][:, 1, :], op0=ALU.mult, op1=ALU.add, accum_out=level[n][:]
+            )
+
+        def RT(n, h):
+            cs = slice(HALF * h, HALF * (h + 1))
+            nc.scalar.activation(
+                out=power[n][:, cs], in_=power[n][:, cs], func=ACT.Abs_reciprocal_sqrt, scale=1024.0, bias=level[n][:]
+            )
+
+        def E(n, h):
+            g, t = divmod(n, PACK)
+            cs = slice(HALF * h, HALF * (h + 1))
+            nc.vector.scalar_tensor_tensor(
+                out=power[n][:, cs], in0=power[n][:, cs], scalar=window_cols[:, g, t : t + 1], in1=gain_bc[:, cs], op0=ALU.mult, op1=ALU.mult
+            )
+
+        def FG(n, h):
+            g, t = divmod(n, PACK)
+            cs = slice(HALF * h, HALF * (h + 1))
+            for ri in range(2):
+                nc.vector.tensor_tensor(out=h_bf[g][ri][:, t, cs], in0=y[(n, ri, h)][:], in1=power[n][:, cs], op=ALU.mult)
+
+        c_codes = [keep.tile([P, 2 * U], U32, name="c_codes%d" % k, align_bytes=64) for k in range(2)]
+        c_scales = [keep.tile([P, 2 * U], U8, name="c_scales%d" % k, align_bytes=64) for k in range(2)]
+        cg = {}
+
+        def c_group(k, gg):
+            cg[(k, gg)] = grp.tile([P, 2048], BF16, name="grouped", align_bytes=64)
+            pe_group(cg[(k, gg)][:], c_raw[k][:, gg], (1, -1)[k])
+
+        def c_quant(k, gg):
+            cs = slice(U * gg, U * (gg + 1))
+            nc.vector.quantize_mx(out=c_codes[k][:, cs].bitcast(FP8X4), scales=c_scales[k][:, cs], in_=cg[(k, gg)][:])
+
+        d_codes = [keep.tile([P, R], U32, name="d_codes%d" % g, align_bytes=64) for g in range(2)]
+        d_scales = [keep.tile([P, R], U8, name="d_scales%d" % g, align_bytes=64) for g in range(2)]
+        dg = {}
+
+        def d_turn(g, qq):
+            if qq == 0:
+                dg[g] = grp.tile([P, 2048], BF16, name="grouped", align_bytes=64)
+            bank = psum.tile([P, 4, P], F32, name="bank", tag="tr", bufs=TB)
+            for k in range(2):
+                words = d_raw[:, 2 * qq + k, :].bitcast(F32)
+                for u in range(2):
+                    nc.tensor.transpose(bank[:, 2 * k + u, :], words[:, 256 * g + u : 256 * (g + 1) : 2], ident[:])
+            nc.scalar.copy(
+                out=dg[g][:, 1024 * qq : 1024 * (qq + 1)].bitcast(F32).rearrange("p (k i u) -> p k i u", k=2, u=2),
+                in_=bank[:].rearrange("p (k u) i -> p k i u", u=2),
+            )
+
+        def d_quant(g):
+            nc.vector.quantize_mx(out=d_codes[g][:].bitcast(FP8X4), scales=d_scales[g][:], in_=dg[g][:])
+
+        z_view = out_0.rearrange("(g p t) v -> g p t v", p=P, t=PACK)
+        hg_t = {}
+        ht = {}
+        zbank = {}
+
+        htb = {}
+
+        def HT(n, ri):
+            g, t = divmod(n, PACK)
+            bank = psum.tile([P, 4, P], F32, name="bank", tag="tr", bufs=TB)
+            words = h_bf[g][ri][:, t, :].bitcast(F32)
+            for gg in range(2):
+                for u in range(2):
+                    nc.tensor.transpose(bank[:, 2 * gg + u, :], words[:, 256 * gg + u : 256 * (gg + 1) : 2], ident[:])
+            htb[(n, ri)] = bank
+
+        def HE(n, ri):
+            if ri == 0:
+                hg_t[n] = grp.tile([P, 2048], BF16, name="grouped", align_bytes=64)
+            nc.scalar.copy(
+                out=hg_t[n][:, 1024 * ri : 1024 * (ri + 1)].bitcast(F32).rearrange("p (k i u) -> p k i u", k=2, u=2),
+                in_=htb[(n, ri)][:].rearrange("p (k u) i -> p k i u", u=2),
+            )
+
+        def HQ(n):
+            codes = lim.tile([P, 512], U32, name="ht_codes", align_bytes=64, bufs=3)
+            scales = lim.tile([P, 512], U8, name="ht_scales", align_bytes=64, bufs=3)
+            nc.vector.quantize_mx(out=codes[:].bitcast(FP8X4), scales=scales[:], in_=hg_t[n][:])
+            ht[n] = (codes, scales)
+
+        def Z(n):
+            codes, scales = ht[n]
+            z = psum.tile([P, U], F32, name="z", tag="tr", bufs=TB)
+            for k in range(4):
+                ri, gg = divmod(k, 2)
+                cs = slice(256 * ri + 128 * gg, 256 * ri + 128 * gg + 128)
+                vs = slice(U * gg, U * (gg + 1))
+                mx(
+                    z[:],
+                    (codes[:, cs].bitcast(FP8X4), scales[:, cs]),
+                    (c_codes[ri][:, vs].bitcast(FP8X4), c_scales[ri][:, vs]),
+                    k == 0,
+                    k == 3,
+                )
+            zbank[n] = z
+
+        def ZE(n):
+            g, t = divmod(n, PACK)
+            z_sb = outp.tile([P, U], F32, name="z_sb")
+            nc.scalar.activation(out=z_sb[:], in_=zbank[n][:], func=ACT.Copy, scale=z_gain_cols[:, g, t : t + 1])
+            nc.sync.dma_start(out=z_view[g][:, t, :], in_=z_sb[:])
+
+        hb_codes = [[keep.tile([P, B], U32, name="hb_codes%d%d" % (g, ri), align_bytes=64) for ri in range(2)] for g in range(2)]
+        hb_scales = [[keep.tile([P, B], U8, name="hb_scales%d%d" % (g, ri), align_bytes=64) for ri in range(2)] for g in range(2)]
+        hbg = {}
+
+        def hb_group(g, ri, h, engine):
+            hbg[(g, ri, h)] = grp.tile([P, 2048], BF16, name="grouped", align_bytes=64)
+            src = h_bf[g][ri][:, :, HALF * h : HALF * (h + 1)]
+            if engine == "t":
+                pe_group(hbg[(g, ri, h)][:], src, 1)
+            else:
+                interleave(engine, hbg[(g, ri, h)][:], src)
+
+        def hb_quant(g, ri, h):
+            cs = slice(HALF * h, HALF * (h + 1))
+            nc.vector.quantize_mx(
+                out=hb_codes[g][ri][:, cs].bitcast(FP8X4), scales=hb_scales[g][ri][:, cs], in_=hbg[(g, ri, h)][:]
+            )
+
+        esq = {}
+
+        def EM(q, h):
+            cs = slice(HALF * h, HALF * (h + 1))
+            rs = slice(P * q, P * (q + 1))
+            esq[(q, h)] = lim.tile([P, 2, HALF], F32, name="sq")
+            for ri in range(2):
+                e = psum.tile([P, HALF], F32, name="y", tag="y", bufs=YB)
+                for g in range(2):
+                    mx(
+                        e[:],
+                        (d_codes[g][:, rs].bitcast(FP8X4), d_scales[g][:, rs]),
+                        (hb_codes[g][ri][:, cs].bitcast(FP8X4), hb_scales[g][ri][:, cs]),
+                        g == 0,
+                        g == 1,
+                    )
+                nc.scalar.activation(out=esq[(q, h)][:, ri, :], in_=e[:], func=ACT.Square)
+
+        total = {}
+
+        def EA(q, h):
+            total[(q, h)] = outp.tile([P, HALF], F32, name="total")
+            nc.vector.tensor_tensor(out=total[(q, h)][:], in0=esq[(q, h)][:, 0, :], in1=esq[(q, h)][:, 1, :], op=ALU.add)
+
+        def EP(q, h):
+            cs = slice(HALF * h, HALF * (h + 1))
+            o = outp.tile([P, HALF], F32, name="o_map", bufs=4)
+            nc.vector.tensor_tensor(out=o[:], in0=total[(q, h)][:], in1=pg2_bc[:, cs], op=ALU.mult)
+            nc.sync.dma_start(out=out_1[P * q : P * (q + 1), cs], in_=o[:])
+
+        broadcast(ones_f[:], scale_rows[:], scale_bc[:], ACT.Copy)
+        s_group(0, 0, "v")
+        s_group(1, 0, "v")
+        s_quant(0, 0)
+        x_turn(0, 1, 0)
+        x_turn(0, 1, 1)
+        s_group(0, 1, "t")
+        x_product(0, (0, 1))
+        x_turn(0, 0, 0)
+        x_product(0, (2, 3))
+        x_turn(0, 0, 1)
+        s_group(1, 1, "s")
+        s_quant(1, 0)
+        s_neg(0)
+        x_quant(0, 1)
+        x_quant(0, 0)
+        s_quant(2, 0)
+        Y(0, 0)
+        SQ(0, 0)
+        nc.vector.tensor_copy(out=window_cols[:], in_=window_bf[:])
+        nc.vector.tensor_copy(out=z_gain_cols[:], in_=z_gain_bf[:])
+        s_quant(0, 1)
+        s_quant(1, 1)
+        s_neg(1)
+        x_product(1, (0, 1))
+        s_quant(2, 1)
+        Y(0, 1)
+        SQ(0, 1)
+
+        def job(f, *a):
+            return lambda: f(*a)
+
+        fill_m = {
+            0: [job(x_product, 1, (2, 3))],
+            1: [job(c_quant, 0, 0)],
+        }
+        fill_v = {
+            0: [],
+            1: [job(c_quant, 0, 1), job(c_quant, 1, 0)],
+            2: [job(c_quant, 1, 1), job(x_quant, 1, 1), job(x_quant, 1, 0)],
+            4: [job(d_quant, 0)],
+            5: [job(d_quant, 1), job(hb_quant, 0, 0, 0)],
+            6: [job(hb_quant, 0, 0, 1)],
+            7: [job(hb_quant, 0, 1, 0), job(hb_quant, 0, 1, 1)],
+        }
+        fill_s = {
+            0: [job(c_group, 0, 0), job(c_group, 0, 1)],
+            1: [job(c_group, 1, 0), job(c_group, 1, 1)],
+            2: [job(x_turn, 1, 1, 0), job(x_turn, 1, 1, 1), job(x_turn, 1, 0, 0), job(x_turn, 1, 0, 1)],
+            3: [job(d_turn, 0, 0), job(d_turn, 0, 1)],
+            4: [job(d_turn, 1, 0), job(d_turn, 1, 1), job(hb_group, 0, 0, 0, "t")],
+            5: [job(hb_group, 0, 0, 1, "t")],
+            6: [job(hb_group, 0, 1, 0, "t")],
+            7: [job(hb_group, 0, 1, 1, "t")],
+        }
+
+        def fill(table, n):
+            for j in table.get(n, []):
+                j()
+
+        for n in range(8):
+            C(n)
+            if n > 1:
+                HE(n - 2, 0)
+                HE(n - 2, 1)
+            RT(n, 0)
+            RT(n, 1)
+            if n > 1:
+                HQ(n - 2)
+            fill(fill_m, n)
+            E(n, 0)
+            if n < 7:
+                Y(n + 1, 0)
+                SQ(n + 1, 0)
+            if n > 2:
+                Z(n - 3)
+                ZE(n - 3)
+            FG(n, 0)
+            fill(fill_s, n)
+            E(n, 1)
+            FG(n, 1)
+            if n < 7:
+                Y(n + 1, 1)
+                SQ(n + 1, 1)
+            if n > 0:
+                HT(n - 1, 0)
+                HT(n - 1, 1)
+            fill(fill_v, n)
+
+        hb_group(1, 0, 0, "v")
+        HE(6, 0)
+        HE(6, 1)
+        hb_group(1, 1, 0, "t")
+        HT(7, 0)
+        HT(7, 1)
+        HE(7, 0)
+        HE(7, 1)
+        hb_quant(1, 0, 0)
+        HQ(6)
+        hb_quant(1, 1, 0)
+        hb_group(1, 0, 1, "v")
+        HQ(7)
+        Z(5)
+        ZE(5)
+        for q in range(4):
+            EM(q, 0)
+            if q == 0:
+                hb_group(1, 1, 1, "t")
+                hb_quant(1, 0, 1)
+            if q == 1:
+                Z(6)
+                ZE(6)
+                hb_quant(1, 1, 1)
+            if q == 2:
+                Z(7)
+                ZE(7)
+            if q > 0:
+                EA(q - 1, 0)
+            if q > 1:
+                EP(q - 2, 0)
+        for q in range(4):
+            EM(q, 1)
+            if q == 0:
+                EA(3, 0)
+                EP(2, 0)
+            if q == 1:
+                EP(3, 0)
+            if q > 0:
+                EA(q - 1, 1)
+            if q > 1:
+                EP(q - 2, 1)
+        EA(3, 1)
+        EP(2, 1)
+        EP(3, 1)

@@ -18,7 +18,7 @@ ALU = mybir.AluOpType
 P = 128
 PACK = 4
 HALF = 512
-YB = 6
+YB = {"y2": 4, "y1": 2}
 TB = 2
 
 
@@ -87,7 +87,6 @@ def tile_limited_beam_combining_f6_kernel(
         p_gain_bc = const.tile([P, B], BF16, name="p_gain_bc")
         nc.sync.dma_start(out=p_gain_bc[:], in_=p_gain.partition_broadcast(P))
         pg2_bc = const.tile([P, B], F32, name="pg2_bc")
-        nc.gpsimd.tensor_tensor(out=pg2_bc[:], in0=p_gain_bc[:], in1=p_gain_bc[:], op=ALU.mult)
 
         def broadcast(lhsT, row, out, func):
             bank = psum.tile([P, HALF], F32, name="bank", tag="tr", bufs=TB)
@@ -187,27 +186,27 @@ def tile_limited_beam_combining_f6_kernel(
         level = {}
         power = {}
 
-        def Y(n, h):
+        def Y(n, h, tag):
             g, t = divmod(n, PACK)
             xr_op, xi_op = x_q[(g, t, 0)], x_q[(g, t, 1)]
-            yr = psum.tile([P, HALF], F32, name="y", tag="y", bufs=YB)
+            yr = psum.tile([P, HALF], F32, name="y", tag=tag, bufs=YB[tag])
             mx(yr[:], xr_op, s_op(0, h), True, False)
             mx(yr[:], xi_op, s_op(1, h), False, True)
-            yi = psum.tile([P, HALF], F32, name="y", tag="y", bufs=YB)
+            yi = psum.tile([P, HALF], F32, name="y", tag=tag, bufs=YB[tag])
             mx(yi[:], xi_op, s_op(0, h), True, False)
             mx(yi[:], xr_op, s_op(2, h), False, True)
             y[(n, 0, h)], y[(n, 1, h)] = yr, yi
 
         def SQ(n, h):
-            if h == 0:
+            if n not in sq:
                 sq[n] = lim.tile([P, 2, B], F32, name="sq")
             cs = slice(HALF * h, HALF * (h + 1))
             for ri in range(2):
                 nc.scalar.activation(out=sq[n][:, ri, cs], in_=y[(n, ri, h)][:], func=ACT.Square, scale=1.0 / 32.0)
 
         def C(n):
-            level[n] = lim.tile([P, 1], F32, name="level")
-            power[n] = lim.tile([P, B], F32, name="power")
+            level[n] = lim.tile([P, 1], F32, name="level", bufs=3)
+            power[n] = lim.tile([P, B], F32, name="power", bufs=3)
             nc.vector.scalar_tensor_tensor(
                 out=power[n][:], in0=sq[n][:, 0, :], scalar=1.0, in1=sq[n][:, 1, :], op0=ALU.mult, op1=ALU.add, accum_out=level[n][:]
             )
@@ -225,19 +224,28 @@ def tile_limited_beam_combining_f6_kernel(
                 out=power[n][:, cs], in0=power[n][:, cs], scalar=window_cols[:, g, t : t + 1], in1=gain_bc[:, cs], op0=ALU.mult, op1=ALU.mult
             )
 
-        def FG(n, h):
+        def FG(n, h, ris=(0, 1)):
             g, t = divmod(n, PACK)
             cs = slice(HALF * h, HALF * (h + 1))
-            for ri in range(2):
+            for ri in ris:
                 nc.vector.tensor_tensor(out=h_bf[g][ri][:, t, cs], in0=y[(n, ri, h)][:], in1=power[n][:, cs], op=ALU.mult)
 
         c_codes = [keep.tile([P, 2 * U], U32, name="c_codes%d" % k, align_bytes=64) for k in range(2)]
         c_scales = [keep.tile([P, 2 * U], U8, name="c_scales%d" % k, align_bytes=64) for k in range(2)]
         cg = {}
 
-        def c_group(k, gg):
-            cg[(k, gg)] = grp.tile([P, 2048], BF16, name="grouped", align_bytes=64)
-            pe_group(cg[(k, gg)][:], c_raw[k][:, gg], (1, -1)[k])
+        def c_group(k, gg, part, engine):
+            if part == 0:
+                cg[(k, gg)] = grp.tile([P, 2048], BF16, name="grouped", align_bytes=64)
+            if engine == "t":
+                pe_group(cg[(k, gg)][:], c_raw[k][:, gg], (1, -1)[k])
+                return
+            o = cg[(k, gg)][:, 1024 * part : 1024 * (part + 1)].rearrange("p (c i t) -> p c t i", i=4, t=PACK)
+            s = c_raw[k][:, gg, :, 256 * part : 256 * (part + 1)].rearrange("p t (c i) -> p c t i", i=4)
+            if engine == "s":
+                nc.scalar.activation(out=o, in_=s, func=ACT.Copy, scale=(1.0, -1.0)[k])
+            else:
+                nc.vector.tensor_scalar(out=o, in0=s, scalar1=(1.0, -1.0)[k], scalar2=None, op0=ALU.mult)
 
         def c_quant(k, gg):
             cs = slice(U * gg, U * (gg + 1))
@@ -279,10 +287,11 @@ def tile_limited_beam_combining_f6_kernel(
                     nc.tensor.transpose(bank[:, 2 * gg + u, :], words[:, 256 * gg + u : 256 * (gg + 1) : 2], ident[:])
             htb[(n, ri)] = bank
 
-        def HE(n, ri):
+        def HE(n, ri, engine="s"):
             if ri == 0:
                 hg_t[n] = grp.tile([P, 2048], BF16, name="grouped", align_bytes=64)
-            nc.scalar.copy(
+            copy = nc.vector.tensor_copy if engine == "v" else nc.scalar.copy
+            copy(
                 out=hg_t[n][:, 1024 * ri : 1024 * (ri + 1)].bitcast(F32).rearrange("p (k i u) -> p k i u", k=2, u=2),
                 in_=htb[(n, ri)][:].rearrange("p (k u) i -> p k i u", u=2),
             )
@@ -319,13 +328,16 @@ def tile_limited_beam_combining_f6_kernel(
         hb_scales = [[keep.tile([P, B], U8, name="hb_scales%d%d" % (g, ri), align_bytes=64) for ri in range(2)] for g in range(2)]
         hbg = {}
 
-        def hb_group(g, ri, h, engine):
-            hbg[(g, ri, h)] = grp.tile([P, 2048], BF16, name="grouped", align_bytes=64)
-            src = h_bf[g][ri][:, :, HALF * h : HALF * (h + 1)]
+        def hb_group(g, ri, h, engine, part=None):
+            if part != 1:
+                hbg[(g, ri, h)] = grp.tile([P, 2048], BF16, name="grouped", align_bytes=64)
+            lo, hi = (0, HALF) if part is None else (256 * part, 256 * (part + 1))
+            src = h_bf[g][ri][:, :, HALF * h + lo : HALF * h + hi]
+            dst = hbg[(g, ri, h)][:, PACK * lo : PACK * hi]
             if engine == "t":
-                pe_group(hbg[(g, ri, h)][:], src, 1)
+                pe_group(dst, src, 1)
             else:
-                interleave(engine, hbg[(g, ri, h)][:], src)
+                interleave(engine, dst, src)
 
         def hb_quant(g, ri, h):
             cs = slice(HALF * h, HALF * (h + 1))
@@ -340,7 +352,7 @@ def tile_limited_beam_combining_f6_kernel(
             rs = slice(P * q, P * (q + 1))
             esq[(q, h)] = lim.tile([P, 2, HALF], F32, name="sq")
             for ri in range(2):
-                e = psum.tile([P, HALF], F32, name="y", tag="y", bufs=YB)
+                e = psum.tile([P, HALF], F32, name="y", tag="y2", bufs=YB["y2"])
                 for g in range(2):
                     mx(
                         e[:],
@@ -369,84 +381,92 @@ def tile_limited_beam_combining_f6_kernel(
         s_quant(0, 0)
         x_turn(0, 1, 0)
         x_turn(0, 1, 1)
-        s_group(0, 1, "t")
+        s_group(0, 1, "s")
         x_product(0, (0, 1))
         x_turn(0, 0, 0)
         x_product(0, (2, 3))
         x_turn(0, 0, 1)
-        s_group(1, 1, "s")
+        s_group(1, 1, "v")
         s_quant(1, 0)
         s_neg(0)
         x_quant(0, 1)
         x_quant(0, 0)
         s_quant(2, 0)
-        Y(0, 0)
+        Y(0, 0, "y1")
         SQ(0, 0)
         nc.vector.tensor_copy(out=window_cols[:], in_=window_bf[:])
         nc.vector.tensor_copy(out=z_gain_cols[:], in_=z_gain_bf[:])
         s_quant(0, 1)
         s_quant(1, 1)
         s_neg(1)
-        x_product(1, (0, 1))
+        Y(1, 0, "y1")
+        SQ(1, 0)
+        x_product(1, (0,))
         s_quant(2, 1)
-        Y(0, 1)
+        x_product(1, (1, 2))
+        Y(0, 1, "y1")
         SQ(0, 1)
+        Y(1, 1, "y1")
+        SQ(1, 1)
+        x_product(1, (3,))
+        C(0)
+        RT(0, 0)
+        RT(0, 1)
+
 
         def job(f, *a):
             return lambda: f(*a)
 
-        fill_m = {
-            0: [job(x_product, 1, (2, 3))],
-            1: [job(c_quant, 0, 0)],
-        }
         fill_v = {
-            0: [],
-            1: [job(c_quant, 0, 1), job(c_quant, 1, 0)],
-            2: [job(c_quant, 1, 1), job(x_quant, 1, 1), job(x_quant, 1, 0)],
-            4: [job(d_quant, 0)],
-            5: [job(d_quant, 1), job(hb_quant, 0, 0, 0)],
-            6: [job(hb_quant, 0, 0, 1)],
-            7: [job(hb_quant, 0, 1, 0), job(hb_quant, 0, 1, 1)],
+            0: [job(c_group, 1, 0, 0, "v"), job(c_group, 1, 0, 1, "v")],
+            1: [job(x_quant, 1, 1), job(x_quant, 1, 0), job(c_quant, 1, 0)],
+            2: [job(c_group, 1, 1, 0, "v"), job(c_group, 1, 1, 1, "v"), job(c_quant, 0, 0)],
+            3: [job(c_quant, 0, 1), job(c_quant, 1, 1)],
+            4: [job(d_quant, 0), job(d_quant, 1), job(hb_group, 0, 0, 0, "v")],
+            5: [job(hb_group, 0, 0, 1, "v"), job(hb_quant, 0, 0, 0)],
+            6: [job(hb_quant, 0, 0, 1), job(hb_quant, 0, 1, 0)],
+            7: [job(hb_quant, 0, 1, 1)],
         }
         fill_s = {
-            0: [job(c_group, 0, 0), job(c_group, 0, 1)],
-            1: [job(c_group, 1, 0), job(c_group, 1, 1)],
-            2: [job(x_turn, 1, 1, 0), job(x_turn, 1, 1, 1), job(x_turn, 1, 0, 0), job(x_turn, 1, 0, 1)],
-            3: [job(d_turn, 0, 0), job(d_turn, 0, 1)],
-            4: [job(d_turn, 1, 0), job(d_turn, 1, 1), job(hb_group, 0, 0, 0, "t")],
-            5: [job(hb_group, 0, 0, 1, "t")],
-            6: [job(hb_group, 0, 1, 0, "t")],
-            7: [job(hb_group, 0, 1, 1, "t")],
+            0: [job(x_turn, 1, 1, 0), job(x_turn, 1, 1, 1), job(x_turn, 1, 0, 0), job(x_turn, 1, 0, 1)],
+            1: [job(c_group, 0, 0, 0, "s"), job(c_group, 0, 0, 1, "s")],
+            2: [job(c_group, 0, 1, 0, "s"), job(c_group, 0, 1, 1, "s")],
+            3: [job(d_turn, 0, 0), job(d_turn, 0, 1), job(d_turn, 1, 0), job(d_turn, 1, 1)],
+            4: [],
+            5: [job(hb_group, 0, 1, 0, "s")],
+            6: [job(hb_group, 0, 1, 1, "s")],
         }
 
         def fill(table, n):
             for j in table.get(n, []):
                 j()
-
         for n in range(8):
-            C(n)
+            if n < 7:
+                C(n + 1)
+            Y(n, 0, "y2")
+            Y(n, 1, "y2")
             if n > 1:
                 HE(n - 2, 0)
                 HE(n - 2, 1)
-            RT(n, 0)
-            RT(n, 1)
+            if n < 7:
+                RT(n + 1, 0)
+                RT(n + 1, 1)
+            E(n, 0)
+            E(n, 1)
             if n > 1:
                 HQ(n - 2)
-            fill(fill_m, n)
-            E(n, 0)
-            if n < 7:
-                Y(n + 1, 0)
-                SQ(n + 1, 0)
-            if n > 2:
-                Z(n - 3)
-                ZE(n - 3)
+            if n < 6:
+                Y(n + 2, 0, "y1")
+                SQ(n + 2, 0)
+            if n > 3:
+                Z(n - 4)
+                ZE(n - 4)
             FG(n, 0)
-            fill(fill_s, n)
-            E(n, 1)
             FG(n, 1)
-            if n < 7:
-                Y(n + 1, 1)
-                SQ(n + 1, 1)
+            if n < 6:
+                Y(n + 2, 1, "y1")
+                SQ(n + 2, 1)
+            fill(fill_s, n)
             if n > 0:
                 HT(n - 1, 0)
                 HT(n - 1, 1)
@@ -455,27 +475,29 @@ def tile_limited_beam_combining_f6_kernel(
         hb_group(1, 0, 0, "v")
         HE(6, 0)
         HE(6, 1)
-        hb_group(1, 1, 0, "t")
         HT(7, 0)
         HT(7, 1)
+        hb_group(1, 1, 0, "s")
         HE(7, 0)
         HE(7, 1)
+        hb_group(1, 0, 1, "v")
         hb_quant(1, 0, 0)
         HQ(6)
+        nc.scalar.activation(out=pg2_bc[:], in_=p_gain_bc[:], func=ACT.Square)
+        hb_group(1, 1, 1, "v")
         hb_quant(1, 1, 0)
-        hb_group(1, 0, 1, "v")
         HQ(7)
+        Z(4)
+        ZE(4)
         Z(5)
         ZE(5)
+        hb_quant(1, 0, 1)
+        hb_quant(1, 1, 1)
         for q in range(4):
             EM(q, 0)
-            if q == 0:
-                hb_group(1, 1, 1, "t")
-                hb_quant(1, 0, 1)
             if q == 1:
                 Z(6)
                 ZE(6)
-                hb_quant(1, 1, 1)
             if q == 2:
                 Z(7)
                 ZE(7)

@@ -55,19 +55,15 @@ def tile_limited_beam_combining_f6_kernel(
         nc.vector.memset(ones_f[:], 1.0)
         warm = const.tile([P, 1], F32, name="warm")
         nc.vector.memset(warm[:], 1.0)
-        ident_b = const.tile([P, P], BF16, name="ident_b")
-        nc.vector.tensor_copy(out=ident_b[:], in_=ident[:])
-        neg_ident_b = const.tile([P, P], BF16, name="neg_ident_b")
-        nc.vector.tensor_scalar(out=neg_ident_b[:], in0=ident[:], scalar1=-1.0, scalar2=None, op0=ALU.mult)
         nc.scalar.dma_start(out=scale_rows[0:1, :], in_=xr_scale)
         for ri in range(2):
             nc.sync.dma_start(out=s_raw[ri][:, :, HALF:B], in_=s_view[ri][:, :, HALF:B])
         gain_bc = const.tile([P, B], BF16, name="gain_bc")
         nc.sync.dma_start(out=gain_bc[:], in_=gain.partition_broadcast(P))
         window_bf = const.tile([P, 2, PACK], BF16, name="window_bf")
-        nc.scalar.dma_start(out=window_bf[:], in_=window.rearrange("(g p t) -> p g t", p=P, t=PACK))
+        nc.sync.dma_start(out=window_bf[:], in_=window.rearrange("(g p t) -> p g t", p=P, t=PACK))
         z_gain_bf = const.tile([P, 2, PACK], BF16, name="z_gain_bf")
-        nc.scalar.dma_start(out=z_gain_bf[:], in_=z_gain.rearrange("(g p t) -> p g t", p=P, t=PACK))
+        nc.sync.dma_start(out=z_gain_bf[:], in_=z_gain.rearrange("(g p t) -> p g t", p=P, t=PACK))
         warm_out = const.tile([P, 1], F32, name="warm_out")
         nc.scalar.activation(out=warm_out[:], in_=warm[:], func=ACT.Abs_reciprocal_sqrt)
 
@@ -98,25 +94,31 @@ def tile_limited_beam_combining_f6_kernel(
         gx = {}
 
         def x_product(g, ts):
-            if ts[0] == 0:
+            if g not in xrb:
                 xrb[g] = xin.tile([P, PACK, A], BF16, name="xrb")
             for t in ts:
                 nc.vector.tensor_tensor(
                     out=xrb[g][:, t, :], in0=x_codes_in[g][:, t, :].bitcast(FP8), in1=scale_bc[:], op=ALU.mult
                 )
 
-        def x_turn(g, ri, pair):
+        xb = {}
+
+        def XT(g, ri, pair):
             src = (xrb, xi_in)[ri][g]
-            if pair == 0:
-                gx[(g, ri)] = grp.tile([P, 2048], BF16, name="grouped", align_bytes=64)
             bank = psum.tile([P, 4, P], F32, name="bank", tag="tr", bufs=TB)
             for tt in range(2):
                 words = src[:, 2 * pair + tt, :].bitcast(F32)
                 for u in range(2):
                     nc.tensor.transpose(bank[:, 2 * tt + u, :], words[:, u : A // 2 : 2], ident[:])
-            nc.scalar.copy(
+            xb[(g, ri, pair)] = bank
+
+        def XE(g, ri, pair, engine="s"):
+            if (g, ri) not in gx:
+                gx[(g, ri)] = grp.tile([P, 2048], BF16, name="grouped", align_bytes=64)
+            copy = nc.vector.tensor_copy if engine == "v" else nc.scalar.copy
+            copy(
                 out=gx[(g, ri)][:, 1024 * pair : 1024 * (pair + 1)].bitcast(F32).rearrange("p (k i u) -> p k i u", k=2, u=2),
-                in_=bank[:].rearrange("p (k u) i -> p k i u", u=2),
+                in_=xb[(g, ri, pair)][:].rearrange("p (k u) i -> p k i u", u=2),
             )
 
         def x_quant(g, ri):
@@ -135,33 +137,17 @@ def tile_limited_beam_combining_f6_kernel(
             else:
                 nc.scalar.copy(out=o, in_=s)
 
-        def pe_group(dst, src, sign):
-            ident_pm = ident_b if sign > 0 else neg_ident_b
-            banks = []
-            for k in range(2):
-                bank = psum.tile([P, 1024], BF16, name="bank", tag="tr", bufs=TB)
-                for m in range(2):
-                    lo = 256 * k + 128 * m
-                    nc.tensor.matmul(
-                        bank[:, 512 * m : 512 * (m + 1)].rearrange("p (c t) -> p c t", t=PACK),
-                        lhsT=ident_pm[:],
-                        rhs=src[:, :, lo : lo + 128].rearrange("p t c -> p c t"),
-                        start=True,
-                        stop=True,
-                    )
-                nc.scalar.copy(out=dst[:, 1024 * k : 1024 * (k + 1)], in_=bank[:])
-
         s_codes = [keep.tile([P, B], U32, name="s_codes%d" % k, align_bytes=64) for k in range(3)]
         s_scales = [keep.tile([P, B], U8, name="s_scales%d" % k, align_bytes=64) for k in range(3)]
         sg = {}
 
         def s_group(ri, h, engine):
             sg[(ri, h)] = grp.tile([P, 2048], BF16, name="grouped", align_bytes=64)
-            src = s_raw[ri][:, :, HALF * h : HALF * (h + 1)]
-            if engine == "t":
-                pe_group(sg[(ri, h)][:], src, 1)
-            else:
-                interleave(engine, sg[(ri, h)][:], src)
+            dst = sg[(ri, h)][:].rearrange("p (u q e t) -> p u q t e", u=2, e=2, t=PACK)
+            src = s_raw[ri][:, :, HALF * h : HALF * (h + 1)].rearrange("p t (q u e) -> p u q t e", u=2, e=2)
+            copy = nc.vector.tensor_copy if engine == "v" else nc.scalar.copy
+            for u in range(2):
+                copy(out=dst[:, u], in_=src[:, u])
 
         def s_neg(h):
             sg[(2, h)] = grp.tile([P, 2048], BF16, name="grouped", align_bytes=64)
@@ -186,23 +172,18 @@ def tile_limited_beam_combining_f6_kernel(
         level = {}
         power = {}
 
-        def Y(n, h, tag):
+        def Y(n, h, ri, tag):
             g, t = divmod(n, PACK)
-            xr_op, xi_op = x_q[(g, t, 0)], x_q[(g, t, 1)]
-            yr = psum.tile([P, HALF], F32, name="y", tag=tag, bufs=YB[tag])
-            mx(yr[:], xr_op, s_op(0, h), True, False)
-            mx(yr[:], xi_op, s_op(1, h), False, True)
-            yi = psum.tile([P, HALF], F32, name="y", tag=tag, bufs=YB[tag])
-            mx(yi[:], xi_op, s_op(0, h), True, False)
-            mx(yi[:], xr_op, s_op(2, h), False, True)
-            y[(n, 0, h)], y[(n, 1, h)] = yr, yi
+            bank = psum.tile([P, HALF], F32, name="y", tag=tag, bufs=YB[tag])
+            mx(bank[:], x_q[(g, t, ri)], s_op(0, h), True, False)
+            mx(bank[:], x_q[(g, t, 1 - ri)], s_op(1 + ri, h), False, True)
+            y[(n, ri, h)] = bank
 
-        def SQ(n, h):
+        def SQ(n, h, ri):
             if n not in sq:
                 sq[n] = lim.tile([P, 2, B], F32, name="sq")
             cs = slice(HALF * h, HALF * (h + 1))
-            for ri in range(2):
-                nc.scalar.activation(out=sq[n][:, ri, cs], in_=y[(n, ri, h)][:], func=ACT.Square, scale=1.0 / 32.0)
+            nc.scalar.activation(out=sq[n][:, ri, cs], in_=y[(n, ri, h)][:], func=ACT.Square, scale=1.0 / 32.0)
 
         def C(n):
             level[n] = lim.tile([P, 1], F32, name="level", bufs=3)
@@ -217,29 +198,31 @@ def tile_limited_beam_combining_f6_kernel(
                 out=power[n][:, cs], in_=power[n][:, cs], func=ACT.Abs_reciprocal_sqrt, scale=1024.0, bias=level[n][:]
             )
 
+        shape = {}
+        gate = const.tile([P, 1], F32, name="gate")
+
         def E(n, h):
+            cs = slice(HALF * h, HALF * (h + 1))
+            shape[(n, h)] = lim.tile([P, HALF], F32, name="shape%d" % h, bufs=1)
+            nc.gpsimd.tensor_tensor(out=shape[(n, h)][:], in0=power[n][:, cs], in1=gain_perm[:, cs], op=ALU.mult)
+
+        def GATE(n):
+            nc.gpsimd.tensor_copy(out=gate[:], in_=level[n][:])
+
+        def FG(n, h, ri):
             g, t = divmod(n, PACK)
             cs = slice(HALF * h, HALF * (h + 1))
             nc.vector.scalar_tensor_tensor(
-                out=power[n][:, cs], in0=power[n][:, cs], scalar=window_cols[:, g, t : t + 1], in1=gain_bc[:, cs], op0=ALU.mult, op1=ALU.mult
+                out=h_bf[g][ri][:, t, cs], in0=y[(n, ri, h)][:], scalar=window_cols[:, g, t : t + 1], in1=shape[(n, h)][:], op0=ALU.mult, op1=ALU.mult
             )
-
-        def FG(n, h, ris=(0, 1)):
-            g, t = divmod(n, PACK)
-            cs = slice(HALF * h, HALF * (h + 1))
-            for ri in ris:
-                nc.vector.tensor_tensor(out=h_bf[g][ri][:, t, cs], in0=y[(n, ri, h)][:], in1=power[n][:, cs], op=ALU.mult)
 
         c_codes = [keep.tile([P, 2 * U], U32, name="c_codes%d" % k, align_bytes=64) for k in range(2)]
         c_scales = [keep.tile([P, 2 * U], U8, name="c_scales%d" % k, align_bytes=64) for k in range(2)]
         cg = {}
 
         def c_group(k, gg, part, engine):
-            if part == 0:
+            if (k, gg) not in cg:
                 cg[(k, gg)] = grp.tile([P, 2048], BF16, name="grouped", align_bytes=64)
-            if engine == "t":
-                pe_group(cg[(k, gg)][:], c_raw[k][:, gg], (1, -1)[k])
-                return
             o = cg[(k, gg)][:, 1024 * part : 1024 * (part + 1)].rearrange("p (c i t) -> p c t i", i=4, t=PACK)
             s = c_raw[k][:, gg, :, 256 * part : 256 * (part + 1)].rearrange("p t (c i) -> p c t i", i=4)
             if engine == "s":
@@ -255,17 +238,23 @@ def tile_limited_beam_combining_f6_kernel(
         d_scales = [keep.tile([P, R], U8, name="d_scales%d" % g, align_bytes=64) for g in range(2)]
         dg = {}
 
-        def d_turn(g, qq):
-            if qq == 0:
-                dg[g] = grp.tile([P, 2048], BF16, name="grouped", align_bytes=64)
+        db = {}
+
+        def DT(g, qq):
             bank = psum.tile([P, 4, P], F32, name="bank", tag="tr", bufs=TB)
             for k in range(2):
                 words = d_raw[:, 2 * qq + k, :].bitcast(F32)
                 for u in range(2):
                     nc.tensor.transpose(bank[:, 2 * k + u, :], words[:, 256 * g + u : 256 * (g + 1) : 2], ident[:])
-            nc.scalar.copy(
+            db[(g, qq)] = bank
+
+        def DE(g, qq, engine="s"):
+            if g not in dg:
+                dg[g] = grp.tile([P, 2048], BF16, name="grouped", align_bytes=64)
+            copy = nc.vector.tensor_copy if engine == "v" else nc.scalar.copy
+            copy(
                 out=dg[g][:, 1024 * qq : 1024 * (qq + 1)].bitcast(F32).rearrange("p (k i u) -> p k i u", k=2, u=2),
-                in_=bank[:].rearrange("p (k u) i -> p k i u", u=2),
+                in_=db[(g, qq)][:].rearrange("p (k u) i -> p k i u", u=2),
             )
 
         def d_quant(g):
@@ -284,11 +273,11 @@ def tile_limited_beam_combining_f6_kernel(
             words = h_bf[g][ri][:, t, :].bitcast(F32)
             for gg in range(2):
                 for u in range(2):
-                    nc.tensor.transpose(bank[:, 2 * gg + u, :], words[:, 256 * gg + u : 256 * (gg + 1) : 2], ident[:])
+                    nc.tensor.transpose(bank[:, 2 * gg + u, :], words[:, 256 * gg + 128 * u : 256 * gg + 128 * (u + 1)], ident[:])
             htb[(n, ri)] = bank
 
         def HE(n, ri, engine="s"):
-            if ri == 0:
+            if n not in hg_t:
                 hg_t[n] = grp.tile([P, 2048], BF16, name="grouped", align_bytes=64)
             copy = nc.vector.tensor_copy if engine == "v" else nc.scalar.copy
             copy(
@@ -297,8 +286,8 @@ def tile_limited_beam_combining_f6_kernel(
             )
 
         def HQ(n):
-            codes = lim.tile([P, 512], U32, name="ht_codes", align_bytes=64, bufs=3)
-            scales = lim.tile([P, 512], U8, name="ht_scales", align_bytes=64, bufs=3)
+            codes = lim.tile([P, 512], U32, name="ht_codes", align_bytes=64, bufs=4)
+            scales = lim.tile([P, 512], U8, name="ht_scales", align_bytes=64, bufs=4)
             nc.vector.quantize_mx(out=codes[:].bitcast(FP8X4), scales=scales[:], in_=hg_t[n][:])
             ht[n] = (codes, scales)
 
@@ -318,10 +307,31 @@ def tile_limited_beam_combining_f6_kernel(
                 )
             zbank[n] = z
 
-        def ZE(n):
+        def PG2():
+            nc.scalar.activation(out=pg2_bc[:], in_=p_gain_bc[:], func=ACT.Square)
+
+        gain_perm = const.tile([P, B], BF16, name="gain_perm")
+
+        def COLS():
+            for h in range(2):
+                cs = slice(HALF * h, HALF * (h + 1))
+                nc.vector.tensor_copy(
+                    out=gain_perm[:, cs].rearrange("p (u q e) -> p u q e", u=2, e=2),
+                    in_=gain_bc[:, cs].rearrange("p (q u e) -> p u q e", u=2, e=2),
+                )
+            nc.vector.tensor_copy(out=window_cols[:], in_=window_bf[:])
+            nc.vector.tensor_copy(out=z_gain_cols[:], in_=z_gain_bf[:])
+
+        def BC():
+            broadcast(ones_f[:], scale_rows[:], scale_bc[:], ACT.Copy)
+
+        def ZE(n, engine="s"):
             g, t = divmod(n, PACK)
             z_sb = outp.tile([P, U], F32, name="z_sb")
-            nc.scalar.activation(out=z_sb[:], in_=zbank[n][:], func=ACT.Copy, scale=z_gain_cols[:, g, t : t + 1])
+            if engine == "s":
+                nc.scalar.activation(out=z_sb[:], in_=zbank[n][:], func=ACT.Copy, scale=z_gain_cols[:, g, t : t + 1])
+            else:
+                nc.vector.tensor_scalar(out=z_sb[:], in0=zbank[n][:], scalar1=z_gain_cols[:, g, t : t + 1], scalar2=None, op0=ALU.mult)
             nc.sync.dma_start(out=z_view[g][:, t, :], in_=z_sb[:])
 
         hb_codes = [[keep.tile([P, B], U32, name="hb_codes%d%d" % (g, ri), align_bytes=64) for ri in range(2)] for g in range(2)]
@@ -329,15 +339,12 @@ def tile_limited_beam_combining_f6_kernel(
         hbg = {}
 
         def hb_group(g, ri, h, engine, part=None):
-            if part != 1:
+            if (g, ri, h) not in hbg:
                 hbg[(g, ri, h)] = grp.tile([P, 2048], BF16, name="grouped", align_bytes=64)
             lo, hi = (0, HALF) if part is None else (256 * part, 256 * (part + 1))
             src = h_bf[g][ri][:, :, HALF * h + lo : HALF * h + hi]
             dst = hbg[(g, ri, h)][:, PACK * lo : PACK * hi]
-            if engine == "t":
-                pe_group(dst, src, 1)
-            else:
-                interleave(engine, dst, src)
+            interleave(engine, dst, src)
 
         def hb_quant(g, ri, h):
             cs = slice(HALF * h, HALF * (h + 1))
@@ -347,21 +354,26 @@ def tile_limited_beam_combining_f6_kernel(
 
         esq = {}
 
-        def EM(q, h):
+        ebank = {}
+
+        def EM(q, h, ri):
             cs = slice(HALF * h, HALF * (h + 1))
             rs = slice(P * q, P * (q + 1))
-            esq[(q, h)] = lim.tile([P, 2, HALF], F32, name="sq")
-            for ri in range(2):
-                e = psum.tile([P, HALF], F32, name="y", tag="y2", bufs=YB["y2"])
-                for g in range(2):
-                    mx(
-                        e[:],
-                        (d_codes[g][:, rs].bitcast(FP8X4), d_scales[g][:, rs]),
-                        (hb_codes[g][ri][:, cs].bitcast(FP8X4), hb_scales[g][ri][:, cs]),
-                        g == 0,
-                        g == 1,
-                    )
-                nc.scalar.activation(out=esq[(q, h)][:, ri, :], in_=e[:], func=ACT.Square)
+            e = psum.tile([P, HALF], F32, name="y", tag="y2", bufs=YB["y2"])
+            for g in range(2):
+                mx(
+                    e[:],
+                    (d_codes[g][:, rs].bitcast(FP8X4), d_scales[g][:, rs]),
+                    (hb_codes[g][ri][:, cs].bitcast(FP8X4), hb_scales[g][ri][:, cs]),
+                    g == 0,
+                    g == 1,
+                )
+            ebank[(q, h, ri)] = e
+
+        def ES(q, h, ri):
+            if (q, h) not in esq:
+                esq[(q, h)] = lim.tile([P, 2, HALF], F32, name="sq")
+            nc.scalar.activation(out=esq[(q, h)][:, ri, :], in_=ebank[(q, h, ri)][:], func=ACT.Square)
 
         total = {}
 
@@ -372,150 +384,371 @@ def tile_limited_beam_combining_f6_kernel(
         def EP(q, h):
             cs = slice(HALF * h, HALF * (h + 1))
             o = outp.tile([P, HALF], F32, name="o_map", bufs=4)
-            nc.vector.tensor_tensor(out=o[:], in0=total[(q, h)][:], in1=pg2_bc[:, cs], op=ALU.mult)
+            nc.vector.tensor_tensor(
+                out=o[:].rearrange("p (q u e) -> p q u e", u=2, e=2),
+                in0=total[(q, h)][:].rearrange("p (u q e) -> p q u e", u=2, e=2),
+                in1=pg2_bc[:, cs].rearrange("p (q u e) -> p q u e", u=2, e=2),
+                op=ALU.mult,
+            )
             nc.sync.dma_start(out=out_1[P * q : P * (q + 1), cs], in_=o[:])
 
-        broadcast(ones_f[:], scale_rows[:], scale_bc[:], ACT.Copy)
-        s_group(0, 0, "v")
+        XT(0, 1, 1)
         s_group(1, 0, "v")
-        s_quant(0, 0)
-        x_turn(0, 1, 0)
-        x_turn(0, 1, 1)
-        s_group(0, 1, "s")
-        x_product(0, (0, 1))
-        x_turn(0, 0, 0)
-        x_product(0, (2, 3))
-        x_turn(0, 0, 1)
-        s_group(1, 1, "v")
-        s_quant(1, 0)
+        s_group(0, 0, "s")
         s_neg(0)
+        XE(0, 1, 1)
+        BC()
+        s_quant(1, 0)
+        s_group(0, 1, "v")
+        x_product(0, (2,))
+        x_product(0, (1,))
+        XT(0, 1, 0)
+        XE(0, 1, 0)
+        x_product(0, (0,))
+        s_group(1, 1, "s")
+        x_product(0, (3,))
+        s_quant(0, 0)
+        XT(0, 0, 0)
+        XT(0, 0, 1)
+        s_quant(2, 0)
+        XE(0, 0, 0)
+        XE(0, 0, 1)
         x_quant(0, 1)
         x_quant(0, 0)
-        s_quant(2, 0)
-        Y(0, 0, "y1")
-        SQ(0, 0)
-        nc.vector.tensor_copy(out=window_cols[:], in_=window_bf[:])
-        nc.vector.tensor_copy(out=z_gain_cols[:], in_=z_gain_bf[:])
-        s_quant(0, 1)
+        Y(0, 0, 1, "y2")
         s_quant(1, 1)
+        Y(0, 0, 0, "y1")
+        s_quant(0, 1)
+        Y(1, 0, 1, "y1")
         s_neg(1)
-        Y(1, 0, "y1")
-        SQ(1, 0)
-        x_product(1, (0,))
-        s_quant(2, 1)
-        x_product(1, (1, 2))
-        Y(0, 1, "y1")
-        SQ(0, 1)
-        Y(1, 1, "y1")
-        SQ(1, 1)
+        SQ(0, 0, 0)
+        SQ(1, 0, 1)
+        Y(0, 0, 0, "y2")
+        Y(0, 1, 0, "y1")
+        Y(0, 0, 1, "y1")
+        SQ(0, 1, 0)
+        SQ(0, 0, 1)
         x_product(1, (3,))
+        s_quant(2, 1)
+        Y(0, 1, 1, "y1")
+        SQ(0, 1, 1)
+        x_product(1, (0,))
+        COLS()
+        x_product(1, (1,))
+        Y(1, 1, 0, "y1")
+        SQ(1, 1, 0)
+        Y(1, 1, 1, "y1")
         C(0)
-        RT(0, 0)
+        x_product(1, (2,))
+        SQ(1, 1, 1)
+        Y(1, 0, 0, "y1")
+        SQ(1, 0, 0)
         RT(0, 1)
-
-
-        def job(f, *a):
-            return lambda: f(*a)
-
-        fill_v = {
-            0: [job(c_group, 1, 0, 0, "v"), job(c_group, 1, 0, 1, "v")],
-            1: [job(x_quant, 1, 1), job(x_quant, 1, 0), job(c_quant, 1, 0)],
-            2: [job(c_group, 1, 1, 0, "v"), job(c_group, 1, 1, 1, "v"), job(c_quant, 0, 0)],
-            3: [job(c_quant, 0, 1), job(c_quant, 1, 1)],
-            4: [job(d_quant, 0), job(d_quant, 1), job(hb_group, 0, 0, 0, "v")],
-            5: [job(hb_group, 0, 0, 1, "v"), job(hb_quant, 0, 0, 0)],
-            6: [job(hb_quant, 0, 0, 1), job(hb_quant, 0, 1, 0)],
-            7: [job(hb_quant, 0, 1, 1)],
-        }
-        fill_s = {
-            0: [job(x_turn, 1, 1, 0), job(x_turn, 1, 1, 1), job(x_turn, 1, 0, 0), job(x_turn, 1, 0, 1)],
-            1: [job(c_group, 0, 0, 0, "s"), job(c_group, 0, 0, 1, "s")],
-            2: [job(c_group, 0, 1, 0, "s"), job(c_group, 0, 1, 1, "s")],
-            3: [job(d_turn, 0, 0), job(d_turn, 0, 1), job(d_turn, 1, 0), job(d_turn, 1, 1)],
-            4: [],
-            5: [job(hb_group, 0, 1, 0, "s")],
-            6: [job(hb_group, 0, 1, 1, "s")],
-        }
-
-        def fill(table, n):
-            for j in table.get(n, []):
-                j()
-        for n in range(8):
-            if n < 7:
-                C(n + 1)
-            Y(n, 0, "y2")
-            Y(n, 1, "y2")
-            if n > 1:
-                HE(n - 2, 0)
-                HE(n - 2, 1)
-            if n < 7:
-                RT(n + 1, 0)
-                RT(n + 1, 1)
-            E(n, 0)
-            E(n, 1)
-            if n > 1:
-                HQ(n - 2)
-            if n < 6:
-                Y(n + 2, 0, "y1")
-                SQ(n + 2, 0)
-            if n > 3:
-                Z(n - 4)
-                ZE(n - 4)
-            FG(n, 0)
-            FG(n, 1)
-            if n < 6:
-                Y(n + 2, 1, "y1")
-                SQ(n + 2, 1)
-            fill(fill_s, n)
-            if n > 0:
-                HT(n - 1, 0)
-                HT(n - 1, 1)
-            fill(fill_v, n)
-
-        hb_group(1, 0, 0, "v")
-        HE(6, 0)
-        HE(6, 1)
-        HT(7, 0)
-        HT(7, 1)
-        hb_group(1, 1, 0, "s")
-        HE(7, 0)
-        HE(7, 1)
-        hb_group(1, 0, 1, "v")
-        hb_quant(1, 0, 0)
+        RT(0, 0)
+        E(0, 0)
+        XT(1, 1, 1)
+        XT(1, 0, 0)
+        Y(2, 1, 0, "y1")
+        C(1)
+        XE(1, 0, 0, "v")
+        Y(2, 1, 1, "y1")
+        XE(1, 1, 1)
+        SQ(2, 1, 0)
+        SQ(2, 1, 1)
+        Y(0, 1, 1, "y2")
+        XT(1, 1, 0)
+        XT(1, 0, 1)
+        XE(1, 1, 0, "v")
+        FG(0, 0, 1)
+        FG(0, 0, 0)
+        Y(2, 0, 0, "y1")
+        Y(2, 0, 1, "y1")
+        c_group(0, 1, 1, "s")
+        RT(1, 0)
+        SQ(2, 0, 0)
+        E(0, 1)
+        c_group(0, 1, 0, "v")
+        GATE(1)
+        RT(1, 1)
+        Y(0, 1, 0, "y2")
+        SQ(2, 0, 1)
+        Y(1, 0, 0, "y2")
+        FG(0, 1, 1)
+        FG(0, 1, 0)
+        Y(1, 0, 1, "y2")
+        E(1, 0)
+        XE(1, 0, 1)
+        Y(3, 1, 0, "y1")
+        C(2)
+        Y(3, 1, 1, "y1")
+        SQ(3, 1, 0)
+        HT(0, 1)
+        HT(0, 0)
+        SQ(3, 1, 1)
+        Y(1, 1, 1, "y2")
+        c_group(0, 0, 1, "s")
+        HE(0, 1, "s")
+        x_quant(1, 0)
+        x_quant(1, 1)
+        HE(0, 0, "v")
+        FG(1, 0, 1)
+        FG(1, 0, 0)
+        Y(3, 0, 0, "y1")
+        Y(3, 0, 1, "y1")
+        c_quant(0, 1)
+        RT(2, 0)
+        HQ(0)
+        SQ(3, 0, 0)
+        E(1, 1)
+        DT(0, 0)
+        GATE(2)
+        RT(2, 1)
+        c_group(0, 0, 0, "v")
+        DE(0, 0)
+        Y(1, 1, 0, "y2")
+        SQ(3, 0, 1)
+        Y(2, 0, 0, "y2")
+        FG(1, 1, 1)
+        c_group(1, 0, 0, "s")
+        FG(1, 1, 0)
+        Y(2, 0, 1, "y2")
+        E(2, 0)
+        Y(4, 1, 0, "y1")
+        C(3)
+        Y(4, 1, 1, "y1")
+        SQ(4, 1, 0)
+        HT(1, 1)
+        HT(1, 0)
+        c_group(1, 1, 1, "v")
+        SQ(4, 1, 1)
+        Y(2, 1, 1, "y2")
+        HE(1, 1, "s")
+        HE(1, 0, "s")
+        FG(2, 0, 1)
+        FG(2, 0, 0)
+        Y(4, 0, 0, "y1")
+        Y(4, 0, 1, "y1")
+        RT(3, 0)
+        DT(0, 1)
+        HQ(1)
+        SQ(4, 0, 0)
+        E(2, 1)
+        GATE(3)
+        RT(3, 1)
+        Y(2, 1, 0, "y2")
+        DE(0, 1)
+        SQ(4, 0, 1)
+        Y(3, 0, 0, "y2")
+        FG(2, 1, 1)
+        FG(2, 1, 0)
+        Y(3, 0, 1, "y2")
+        E(3, 0)
+        c_group(1, 0, 1, "s")
+        c_quant(0, 0)
+        Y(5, 1, 0, "y1")
+        C(4)
+        Y(5, 1, 1, "y1")
+        SQ(5, 1, 0)
+        d_quant(0)
+        HT(2, 1)
+        HT(2, 0)
+        SQ(5, 1, 1)
+        Y(3, 1, 1, "y2")
+        HE(2, 1, "s")
+        HE(2, 0, "s")
+        FG(3, 0, 1)
+        FG(3, 0, 0)
+        Y(5, 0, 0, "y1")
+        hb_group(0, 1, 0, "v")
+        Y(5, 0, 1, "y1")
+        c_group(1, 1, 0, "s")
+        RT(4, 0)
+        HQ(2)
+        DT(1, 1)
+        SQ(5, 0, 0)
+        E(3, 1)
+        GATE(4)
+        RT(4, 1)
+        DT(1, 0)
+        Y(3, 1, 0, "y2")
+        SQ(5, 0, 1)
+        Y(4, 0, 0, "y2")
+        FG(3, 1, 1)
+        FG(3, 1, 0)
+        Y(4, 0, 1, "y2")
+        E(4, 0)
+        c_quant(1, 0)
+        Y(6, 1, 0, "y1")
+        C(5)
+        DE(1, 0)
+        DE(1, 1)
+        Y(6, 1, 1, "y1")
+        c_quant(1, 1)
+        SQ(6, 1, 0)
+        HT(3, 1)
+        HT(3, 0)
+        SQ(6, 1, 1)
+        Y(4, 1, 1, "y2")
+        HE(3, 1, "s")
+        HE(3, 0, "s")
+        FG(4, 0, 1)
+        FG(4, 0, 0)
+        Y(6, 0, 0, "y1")
+        hb_group(0, 1, 1, "v")
+        Y(6, 0, 1, "y1")
+        Z(0)
+        hb_quant(0, 1, 0)
+        RT(5, 0)
+        HQ(3)
+        SQ(6, 0, 0)
+        E(4, 1)
+        GATE(5)
+        RT(5, 1)
+        Y(4, 1, 0, "y2")
+        hb_quant(0, 1, 1)
+        SQ(6, 0, 1)
+        Y(5, 0, 0, "y2")
+        FG(4, 1, 1)
+        FG(4, 1, 0)
+        Y(5, 0, 1, "y2")
+        E(5, 0)
+        ZE(0)
+        Y(7, 1, 0, "y1")
+        d_quant(1)
+        C(6)
+        hb_group(0, 0, 1, "s")
+        Y(7, 1, 1, "y1")
+        SQ(7, 1, 0)
+        HT(4, 1)
+        HT(4, 0)
+        SQ(7, 1, 1)
+        Y(5, 1, 1, "y2")
+        HE(4, 1, "s")
+        HE(4, 0, "s")
+        FG(5, 0, 1)
+        FG(5, 0, 0)
+        Y(7, 0, 0, "y1")
+        Y(7, 0, 1, "y1")
+        Z(1)
+        hb_quant(0, 0, 1)
+        RT(6, 0)
+        HQ(4)
+        SQ(7, 0, 0)
+        E(5, 1)
+        GATE(6)
+        RT(6, 1)
+        Y(5, 1, 0, "y2")
+        SQ(7, 0, 1)
+        Y(6, 0, 0, "y2")
+        FG(5, 1, 1)
+        FG(5, 1, 0)
+        Y(6, 0, 1, "y2")
+        E(6, 0)
+        ZE(1)
+        C(7)
+        HT(5, 1)
+        HT(5, 0)
+        Y(6, 1, 1, "y2")
+        HE(5, 1, "s")
+        HE(5, 0, "s")
+        FG(6, 0, 1)
+        FG(6, 0, 0)
+        Z(2)
+        RT(7, 0)
+        HQ(5)
+        E(6, 1)
+        GATE(7)
+        RT(7, 1)
+        Y(6, 1, 0, "y2")
+        hb_group(0, 0, 0, "s")
+        Y(7, 0, 0, "y2")
+        FG(6, 1, 1)
+        FG(6, 1, 0)
+        Y(7, 0, 1, "y2")
+        E(7, 0)
+        ZE(2, "v")
+        HT(6, 1)
+        HT(6, 0)
+        Y(7, 1, 1, "y2")
+        HE(6, 1, "s")
+        HE(6, 0, "s")
+        FG(7, 0, 1)
+        FG(7, 0, 0)
+        hb_quant(0, 0, 0)
+        Z(3)
         HQ(6)
-        nc.scalar.activation(out=pg2_bc[:], in_=p_gain_bc[:], func=ACT.Square)
-        hb_group(1, 1, 1, "v")
-        hb_quant(1, 1, 0)
-        HQ(7)
-        Z(4)
-        ZE(4)
+        E(7, 1)
+        Y(7, 1, 0, "y2")
+        FG(7, 1, 1)
+        FG(7, 1, 0)
+        ZE(3)
         Z(5)
+        hb_group(1, 1, 0, "s")
+        hb_group(1, 0, 0, "v")
+        HT(7, 0)
+        hb_quant(1, 0, 0)
+        PG2()
+        hb_quant(1, 1, 0)
         ZE(5)
+        EM(1, 0, 0)
+        ES(1, 0, 0)
+        EM(2, 0, 0)
+        EM(2, 0, 1)
+        ES(2, 0, 0)
+        EM(1, 0, 1)
+        hb_group(1, 0, 1, "v")
+        EM(0, 0, 1)
+        Z(4)
+        EM(0, 0, 0)
+        HE(7, 0, "s")
+        hb_group(1, 1, 1, "v")
+        ES(1, 0, 1)
+        ES(2, 0, 1)
         hb_quant(1, 0, 1)
+        ZE(4)
+        EM(0, 1, 0)
+        EA(1, 0)
+        ES(0, 0, 1)
+        EM(3, 0, 0)
         hb_quant(1, 1, 1)
-        for q in range(4):
-            EM(q, 0)
-            if q == 1:
-                Z(6)
-                ZE(6)
-            if q == 2:
-                Z(7)
-                ZE(7)
-            if q > 0:
-                EA(q - 1, 0)
-            if q > 1:
-                EP(q - 2, 0)
-        for q in range(4):
-            EM(q, 1)
-            if q == 0:
-                EA(3, 0)
-                EP(2, 0)
-            if q == 1:
-                EP(3, 0)
-            if q > 0:
-                EA(q - 1, 1)
-            if q > 1:
-                EP(q - 2, 1)
+        EA(2, 0)
+        ES(0, 0, 0)
+        EM(0, 1, 1)
+        EM(3, 1, 0)
+        HT(7, 1)
+        ES(0, 1, 0)
+        ES(0, 1, 1)
+        EM(3, 0, 1)
+        EP(1, 0)
+        EA(0, 0)
+        ES(3, 0, 0)
+        Z(6)
+        EP(2, 0)
+        HE(7, 1, "s")
+        EP(0, 0)
+        ES(3, 0, 1)
+        EA(0, 1)
+        EM(3, 1, 1)
+        ES(3, 1, 0)
+        EM(1, 1, 0)
+        EM(1, 1, 1)
+        HQ(7)
+        EA(3, 0)
+        ES(3, 1, 1)
+        EP(0, 1)
         EA(3, 1)
-        EP(2, 1)
+        EP(3, 0)
+        EM(2, 1, 0)
+        ES(1, 1, 0)
+        ES(1, 1, 1)
+        ES(2, 1, 0)
+        EM(2, 1, 1)
+        ES(2, 1, 1)
         EP(3, 1)
+        ZE(6)
+        EA(1, 1)
+        Z(7)
+        ZE(7)
+        EA(2, 1)
+        EP(1, 1)
+        EP(2, 1)

@@ -43,10 +43,6 @@ def tile_limited_beam_combining_f6_kernel(
         xi_in = [xin.tile([P, PACK, A], BF16, name="xi_in") for g in range(2)]
         s_raw = [rawp.tile([P, PACK, B], BF16, name="raw") for ri in range(2)]
         s_view = [src.rearrange("(p j) w -> p j w", j=PACK) for src in (sr, si)]
-        for ri in range(2):
-            nc.sync.dma_start(out=s_raw[ri][:, :, 0:HALF], in_=s_view[ri][:, :, 0:HALF])
-        nc.sync.dma_start(out=x_codes_in[0][:], in_=xr_view[0])
-        nc.sync.dma_start(out=xi_in[0][:], in_=xi_view[0])
         scale_rows = const.tile([P, A], F32, name="scale_rows")
         nc.gpsimd.memset(scale_rows[:], 0.0)
         ident = const.tile([P, P], F32, name="ident")
@@ -55,33 +51,50 @@ def tile_limited_beam_combining_f6_kernel(
         nc.vector.memset(ones_f[:], 1.0)
         warm = const.tile([P, 1], F32, name="warm")
         nc.vector.memset(warm[:], 1.0)
-        nc.scalar.dma_start(out=scale_rows[0:1, :], in_=xr_scale)
-        for ri in range(2):
-            nc.sync.dma_start(out=s_raw[ri][:, :, HALF:B], in_=s_view[ri][:, :, HALF:B])
         gain_bc = const.tile([P, B], BF16, name="gain_bc")
-        nc.sync.dma_start(out=gain_bc[:], in_=gain.partition_broadcast(P))
         window_bf = const.tile([P, 2, PACK], BF16, name="window_bf")
-        nc.sync.dma_start(out=window_bf[:], in_=window.rearrange("(g p t) -> p g t", p=P, t=PACK))
         z_gain_bf = const.tile([P, 2, PACK], BF16, name="z_gain_bf")
-        nc.sync.dma_start(out=z_gain_bf[:], in_=z_gain.rearrange("(g p t) -> p g t", p=P, t=PACK))
-        warm_out = const.tile([P, 1], F32, name="warm_out")
-        nc.scalar.activation(out=warm_out[:], in_=warm[:], func=ACT.Abs_reciprocal_sqrt)
+        p_gain_bc = const.tile([P, B], BF16, name="p_gain_bc")
+        c_raw = {}
+        d_raw = {}
 
-        nc.sync.dma_start(out=x_codes_in[1][:], in_=xr_view[1])
-        nc.sync.dma_start(out=xi_in[1][:], in_=xi_view[1])
-        c_raw = []
-        for src in (cr, ci):
-            raw = rawp.tile([P, 2, PACK, U], BF16, name="raw")
-            nc.sync.dma_start(out=raw[:], in_=src.rearrange("(g p j) v -> p g j v", p=P, j=PACK))
-            c_raw.append(raw)
-        d_raw = rawp.tile([P, 4, T], BF16, name="raw")
-        nc.sync.dma_start(out=d_raw[:], in_=d.rearrange("(q p) i -> p q i", p=P))
+        def LD_scale():
+            nc.scalar.dma_start(out=scale_rows[0:1, :], in_=xr_scale)
+            warm_out = const.tile([P, 1], F32, name="warm_out")
+            nc.scalar.activation(out=warm_out[:], in_=warm[:], func=ACT.Abs_reciprocal_sqrt)
+
+        def LD_s(ri, h):
+            cs = slice(HALF * h, HALF * (h + 1))
+            nc.sync.dma_start(out=s_raw[ri][:, :, cs], in_=s_view[ri][:, :, cs])
+
+        def LD_x(g, ri, pair):
+            ts = slice(2 * pair, 2 * pair + 2)
+            if ri == 0:
+                nc.sync.dma_start(out=x_codes_in[g][:, ts, :], in_=xr_view[g][:, ts, :])
+            else:
+                nc.sync.dma_start(out=xi_in[g][:, ts, :], in_=xi_view[g][:, ts, :])
+
+        def LD_gain():
+            nc.sync.dma_start(out=gain_bc[:], in_=gain.partition_broadcast(P))
+
+        def LD_cols():
+            nc.sync.dma_start(out=window_bf[:], in_=window.rearrange("(g p t) -> p g t", p=P, t=PACK))
+            nc.sync.dma_start(out=z_gain_bf[:], in_=z_gain.rearrange("(g p t) -> p g t", p=P, t=PACK))
+
+        def LD_c(k):
+            c_raw[k] = rawp.tile([P, 2, PACK, U], BF16, name="raw")
+            nc.sync.dma_start(out=c_raw[k][:], in_=(cr, ci)[k].rearrange("(g p j) v -> p g j v", p=P, j=PACK))
+
+        def LD_d():
+            d_raw[0] = rawp.tile([P, 4, T], BF16, name="raw")
+            nc.sync.dma_start(out=d_raw[0][:], in_=d.rearrange("(q p) i -> p q i", p=P))
+
+        def LD_pg():
+            nc.sync.dma_start(out=p_gain_bc[:], in_=p_gain.partition_broadcast(P))
 
         window_cols = const.tile([P, 2, PACK], F32, name="window_cols")
         z_gain_cols = const.tile([P, 2, PACK], F32, name="z_gain_cols")
         scale_bc = const.tile([P, A], F32, name="scale_bc")
-        p_gain_bc = const.tile([P, B], BF16, name="p_gain_bc")
-        nc.sync.dma_start(out=p_gain_bc[:], in_=p_gain.partition_broadcast(P))
         pg2_bc = const.tile([P, B], F32, name="pg2_bc")
 
         def broadcast(lhsT, row, out, func):
@@ -177,13 +190,13 @@ def tile_limited_beam_combining_f6_kernel(
             bank = psum.tile([P, HALF], F32, name="y", tag=tag, bufs=YB[tag])
             mx(bank[:], x_q[(g, t, ri)], s_op(0, h), True, False)
             mx(bank[:], x_q[(g, t, 1 - ri)], s_op(1 + ri, h), False, True)
-            y[(n, ri, h)] = bank
+            y[(n, ri, h, tag)] = bank
 
         def SQ(n, h, ri):
             if n not in sq:
                 sq[n] = lim.tile([P, 2, B], F32, name="sq")
             cs = slice(HALF * h, HALF * (h + 1))
-            nc.scalar.activation(out=sq[n][:, ri, cs], in_=y[(n, ri, h)][:], func=ACT.Square, scale=1.0 / 32.0)
+            nc.scalar.activation(out=sq[n][:, ri, cs], in_=y[(n, ri, h, "y1")][:], func=ACT.Square, scale=1.0 / 32.0)
 
         def C(n):
             level[n] = lim.tile([P, 1], F32, name="level", bufs=3)
@@ -198,23 +211,17 @@ def tile_limited_beam_combining_f6_kernel(
                 out=power[n][:, cs], in_=power[n][:, cs], func=ACT.Abs_reciprocal_sqrt, scale=1024.0, bias=level[n][:]
             )
 
-        shape = {}
-        gate = const.tile([P, 1], F32, name="gate")
-
         def E(n, h):
+            g, t = divmod(n, PACK)
             cs = slice(HALF * h, HALF * (h + 1))
-            shape[(n, h)] = lim.tile([P, HALF], F32, name="shape%d" % h, bufs=1)
-            nc.gpsimd.tensor_tensor(out=shape[(n, h)][:], in0=power[n][:, cs], in1=gain_perm[:, cs], op=ALU.mult)
-
-        def GATE(n):
-            nc.gpsimd.tensor_copy(out=gate[:], in_=level[n][:])
+            nc.vector.scalar_tensor_tensor(
+                out=power[n][:, cs], in0=power[n][:, cs], scalar=window_cols[:, g, t : t + 1], in1=gain_perm[:, cs], op0=ALU.mult, op1=ALU.mult
+            )
 
         def FG(n, h, ri):
             g, t = divmod(n, PACK)
             cs = slice(HALF * h, HALF * (h + 1))
-            nc.vector.scalar_tensor_tensor(
-                out=h_bf[g][ri][:, t, cs], in0=y[(n, ri, h)][:], scalar=window_cols[:, g, t : t + 1], in1=shape[(n, h)][:], op0=ALU.mult, op1=ALU.mult
-            )
+            nc.vector.tensor_tensor(out=h_bf[g][ri][:, t, cs], in0=y[(n, ri, h, "y2")][:], in1=power[n][:, cs], op=ALU.mult)
 
         c_codes = [keep.tile([P, 2 * U], U32, name="c_codes%d" % k, align_bytes=64) for k in range(2)]
         c_scales = [keep.tile([P, 2 * U], U8, name="c_scales%d" % k, align_bytes=64) for k in range(2)]
@@ -243,7 +250,7 @@ def tile_limited_beam_combining_f6_kernel(
         def DT(g, qq):
             bank = psum.tile([P, 4, P], F32, name="bank", tag="tr", bufs=TB)
             for k in range(2):
-                words = d_raw[:, 2 * qq + k, :].bitcast(F32)
+                words = d_raw[0][:, 2 * qq + k, :].bitcast(F32)
                 for u in range(2):
                     nc.tensor.transpose(bank[:, 2 * k + u, :], words[:, 256 * g + u : 256 * (g + 1) : 2], ident[:])
             db[(g, qq)] = bank
@@ -392,363 +399,375 @@ def tile_limited_beam_combining_f6_kernel(
             )
             nc.sync.dma_start(out=out_1[P * q : P * (q + 1), cs], in_=o[:])
 
-        XT(0, 1, 1)
+        LD_scale()
+        LD_s(1, 0)
+        LD_x(0, 0, 1)
         s_group(1, 0, "v")
-        s_group(0, 0, "s")
-        s_neg(0)
-        XE(0, 1, 1)
-        BC()
         s_quant(1, 0)
-        s_group(0, 1, "v")
-        x_product(0, (2,))
+        LD_x(0, 1, 1)
+        LD_x(0, 1, 0)
+        LD_s(0, 0)
+        LD_x(0, 0, 0)
+        BC()
+        x_product(0, (3,))
+        s_neg(0)
+        XT(0, 1, 1)
+        XE(0, 1, 1)
+        x_product(0, (0,))
         x_product(0, (1,))
         XT(0, 1, 0)
+        LD_s(1, 1)
+        x_product(0, (2,))
         XE(0, 1, 0)
-        x_product(0, (0,))
-        s_group(1, 1, "s")
-        x_product(0, (3,))
-        s_quant(0, 0)
+        LD_s(0, 1)
+        x_quant(0, 1)
+        s_group(0, 0, "s")
         XT(0, 0, 0)
         XT(0, 0, 1)
-        s_quant(2, 0)
         XE(0, 0, 0)
+        LD_cols()
+        LD_x(1, 0, 1)
+        s_quant(0, 0)
+        s_quant(2, 0)
         XE(0, 0, 1)
-        x_quant(0, 1)
         x_quant(0, 0)
-        Y(0, 0, 1, "y2")
-        s_quant(1, 1)
-        Y(0, 0, 0, "y1")
-        s_quant(0, 1)
-        Y(1, 0, 1, "y1")
-        s_neg(1)
-        SQ(0, 0, 0)
-        SQ(1, 0, 1)
-        Y(0, 0, 0, "y2")
-        Y(0, 1, 0, "y1")
+        s_group(0, 1, "v")
         Y(0, 0, 1, "y1")
-        SQ(0, 1, 0)
+        s_group(1, 1, "s")
+        LD_c(1)
+        Y(0, 0, 0, "y2")
         SQ(0, 0, 1)
-        x_product(1, (3,))
+        LD_pg()
+        Y(1, 0, 0, "y1")
+        Y(0, 0, 1, "y2")
+        s_neg(1)
+        s_quant(0, 1)
+        Y(0, 0, 0, "y1")
+        SQ(1, 0, 0)
         s_quant(2, 1)
+        SQ(0, 0, 0)
+        s_quant(1, 1)
         Y(0, 1, 1, "y1")
+        LD_x(1, 0, 0)
+        LD_x(1, 1, 0)
         SQ(0, 1, 1)
+        x_product(1, (2,))
         x_product(1, (0,))
-        COLS()
-        x_product(1, (1,))
+        Y(0, 1, 0, "y1")
+        Y(1, 1, 1, "y1")
+        SQ(0, 1, 0)
+        C(0)
+        SQ(1, 1, 1)
         Y(1, 1, 0, "y1")
         SQ(1, 1, 0)
-        Y(1, 1, 1, "y1")
-        C(0)
-        x_product(1, (2,))
-        SQ(1, 1, 1)
-        Y(1, 0, 0, "y1")
-        SQ(1, 0, 0)
-        RT(0, 1)
         RT(0, 0)
+        LD_gain()
+        LD_x(1, 1, 1)
+        LD_c(0)
+        Y(1, 0, 1, "y1")
+        x_product(1, (1,))
+        COLS()
+        SQ(1, 0, 1)
+        x_product(1, (3,))
+        RT(0, 1)
+        LD_d()
+        E(0, 1)
+        Y(0, 1, 1, "y2")
         E(0, 0)
-        XT(1, 1, 1)
-        XT(1, 0, 0)
         Y(2, 1, 0, "y1")
-        C(1)
-        XE(1, 0, 0, "v")
         Y(2, 1, 1, "y1")
-        XE(1, 1, 1)
+        XT(1, 1, 0)
         SQ(2, 1, 0)
         SQ(2, 1, 1)
-        Y(0, 1, 1, "y2")
-        XT(1, 1, 0)
-        XT(1, 0, 1)
-        XE(1, 1, 0, "v")
-        FG(0, 0, 1)
-        FG(0, 0, 0)
-        Y(2, 0, 0, "y1")
-        Y(2, 0, 1, "y1")
-        c_group(0, 1, 1, "s")
-        RT(1, 0)
-        SQ(2, 0, 0)
-        E(0, 1)
-        c_group(0, 1, 0, "v")
-        GATE(1)
-        RT(1, 1)
+        XT(1, 1, 1)
+        XE(1, 1, 0)
+        C(1)
+        FG(0, 1, 1)
+        XT(1, 0, 0)
         Y(0, 1, 0, "y2")
+        c_group(1, 1, 0, "v")
+        FG(0, 0, 0)
+        c_group(1, 0, 1, "s")
+        FG(0, 0, 1)
+        Y(2, 0, 0, "y1")
+        RT(1, 0)
+        RT(1, 1)
+        SQ(2, 0, 0)
+        FG(0, 1, 0)
+        Y(2, 0, 1, "y1")
+        XE(1, 1, 1)
         SQ(2, 0, 1)
         Y(1, 0, 0, "y2")
-        FG(0, 1, 1)
-        FG(0, 1, 0)
         Y(1, 0, 1, "y2")
-        E(1, 0)
-        XE(1, 0, 1)
-        Y(3, 1, 0, "y1")
-        C(2)
-        Y(3, 1, 1, "y1")
-        SQ(3, 1, 0)
-        HT(0, 1)
-        HT(0, 0)
-        SQ(3, 1, 1)
-        Y(1, 1, 1, "y2")
-        c_group(0, 0, 1, "s")
-        HE(0, 1, "s")
-        x_quant(1, 0)
-        x_quant(1, 1)
-        HE(0, 0, "v")
-        FG(1, 0, 1)
-        FG(1, 0, 0)
-        Y(3, 0, 0, "y1")
-        Y(3, 0, 1, "y1")
-        c_quant(0, 1)
-        RT(2, 0)
-        HQ(0)
-        SQ(3, 0, 0)
+        XE(1, 0, 0, "v")
         E(1, 1)
-        DT(0, 0)
-        GATE(2)
-        RT(2, 1)
-        c_group(0, 0, 0, "v")
-        DE(0, 0)
+        Y(1, 1, 1, "y2")
+        E(1, 0)
+        Y(3, 1, 0, "y1")
+        Y(3, 1, 1, "y1")
+        c_group(1, 0, 0, "s")
+        HT(0, 1)
+        SQ(3, 1, 0)
+        SQ(3, 1, 1)
+        HT(0, 0)
+        HE(0, 1, "s")
+        HE(0, 0, "s")
+        C(2)
+        FG(1, 1, 1)
         Y(1, 1, 0, "y2")
+        FG(1, 0, 0)
+        c_group(1, 1, 1, "v")
+        DT(1, 1)
+        FG(1, 0, 1)
+        XT(1, 0, 1)
+        x_quant(1, 1)
+        Y(3, 0, 0, "y1")
+        RT(2, 0)
+        RT(2, 1)
+        XE(1, 0, 1)
+        SQ(3, 0, 0)
+        FG(1, 1, 0)
+        DE(1, 1)
+        x_quant(1, 0)
+        Y(3, 0, 1, "y1")
+        HQ(0)
+        c_quant(1, 1)
         SQ(3, 0, 1)
         Y(2, 0, 0, "y2")
-        FG(1, 1, 1)
-        c_group(1, 0, 0, "s")
-        FG(1, 1, 0)
         Y(2, 0, 1, "y2")
+        E(2, 1)
+        Y(2, 1, 1, "y2")
         E(2, 0)
         Y(4, 1, 0, "y1")
-        C(3)
+        c_group(0, 0, 0, "s")
         Y(4, 1, 1, "y1")
-        SQ(4, 1, 0)
+        c_group(0, 0, 1, "s")
         HT(1, 1)
-        HT(1, 0)
-        c_group(1, 1, 1, "v")
+        SQ(4, 1, 0)
         SQ(4, 1, 1)
-        Y(2, 1, 1, "y2")
+        HT(1, 0)
         HE(1, 1, "s")
+        c_quant(1, 0)
         HE(1, 0, "s")
-        FG(2, 0, 1)
-        FG(2, 0, 0)
-        Y(4, 0, 0, "y1")
-        Y(4, 0, 1, "y1")
-        RT(3, 0)
-        DT(0, 1)
-        HQ(1)
-        SQ(4, 0, 0)
-        E(2, 1)
-        GATE(3)
-        RT(3, 1)
+        C(3)
+        FG(2, 1, 1)
         Y(2, 1, 0, "y2")
-        DE(0, 1)
+        FG(2, 0, 0)
+        FG(2, 0, 1)
+        Y(4, 0, 0, "y1")
+        DT(1, 0)
+        RT(3, 0)
+        RT(3, 1)
+        SQ(4, 0, 0)
+        FG(2, 1, 0)
+        Y(4, 0, 1, "y1")
+        HQ(1)
         SQ(4, 0, 1)
         Y(3, 0, 0, "y2")
-        FG(2, 1, 1)
-        FG(2, 1, 0)
+        c_group(0, 1, 1, "s")
         Y(3, 0, 1, "y2")
-        E(3, 0)
-        c_group(1, 0, 1, "s")
-        c_quant(0, 0)
-        Y(5, 1, 0, "y1")
-        C(4)
-        Y(5, 1, 1, "y1")
-        SQ(5, 1, 0)
-        d_quant(0)
-        HT(2, 1)
-        HT(2, 0)
-        SQ(5, 1, 1)
+        DE(1, 0)
+        E(3, 1)
         Y(3, 1, 1, "y2")
+        E(3, 0)
+        Y(5, 1, 0, "y1")
+        c_quant(0, 0)
+        Y(5, 1, 1, "y1")
+        HT(2, 1)
+        SQ(5, 1, 0)
+        SQ(5, 1, 1)
+        HT(2, 0)
         HE(2, 1, "s")
         HE(2, 0, "s")
-        FG(3, 0, 1)
-        FG(3, 0, 0)
-        Y(5, 0, 0, "y1")
-        hb_group(0, 1, 0, "v")
-        Y(5, 0, 1, "y1")
-        c_group(1, 1, 0, "s")
-        RT(4, 0)
-        HQ(2)
-        DT(1, 1)
-        SQ(5, 0, 0)
-        E(3, 1)
-        GATE(4)
-        RT(4, 1)
-        DT(1, 0)
+        C(4)
+        FG(3, 1, 1)
         Y(3, 1, 0, "y2")
+        FG(3, 0, 0)
+        FG(3, 0, 1)
+        Y(5, 0, 0, "y1")
+        RT(4, 0)
+        RT(4, 1)
+        SQ(5, 0, 0)
+        FG(3, 1, 0)
+        Y(5, 0, 1, "y1")
+        HQ(2)
         SQ(5, 0, 1)
         Y(4, 0, 0, "y2")
-        FG(3, 1, 1)
-        FG(3, 1, 0)
+        DT(0, 0)
+        DT(0, 1)
         Y(4, 0, 1, "y2")
-        E(4, 0)
-        c_quant(1, 0)
-        Y(6, 1, 0, "y1")
-        C(5)
-        DE(1, 0)
-        DE(1, 1)
-        Y(6, 1, 1, "y1")
-        c_quant(1, 1)
-        SQ(6, 1, 0)
-        HT(3, 1)
-        HT(3, 0)
-        SQ(6, 1, 1)
+        d_quant(1)
+        E(4, 1)
         Y(4, 1, 1, "y2")
+        c_group(0, 1, 0, "s")
+        DE(0, 0)
+        E(4, 0)
+        Y(6, 1, 0, "y1")
+        DE(0, 1)
+        Y(6, 1, 1, "y1")
+        HT(3, 1)
+        SQ(6, 1, 0)
+        SQ(6, 1, 1)
+        HT(3, 0)
+        c_quant(0, 1)
         HE(3, 1, "s")
         HE(3, 0, "s")
-        FG(4, 0, 1)
-        FG(4, 0, 0)
-        Y(6, 0, 0, "y1")
+        C(5)
         hb_group(0, 1, 1, "v")
-        Y(6, 0, 1, "y1")
-        Z(0)
-        hb_quant(0, 1, 0)
-        RT(5, 0)
-        HQ(3)
-        SQ(6, 0, 0)
-        E(4, 1)
-        GATE(5)
-        RT(5, 1)
-        Y(4, 1, 0, "y2")
-        hb_quant(0, 1, 1)
-        SQ(6, 0, 1)
-        Y(5, 0, 0, "y2")
         FG(4, 1, 1)
+        Y(4, 1, 0, "y2")
+        FG(4, 0, 0)
+        FG(4, 0, 1)
+        Y(6, 0, 0, "y1")
+        RT(5, 0)
+        RT(5, 1)
+        Z(0)
+        SQ(6, 0, 0)
         FG(4, 1, 0)
-        Y(5, 0, 1, "y2")
-        E(5, 0)
         ZE(0)
-        Y(7, 1, 0, "y1")
-        d_quant(1)
-        C(6)
-        hb_group(0, 0, 1, "s")
-        Y(7, 1, 1, "y1")
-        SQ(7, 1, 0)
-        HT(4, 1)
-        HT(4, 0)
-        SQ(7, 1, 1)
+        Y(6, 0, 1, "y1")
+        HQ(3)
+        d_quant(0)
+        SQ(6, 0, 1)
+        hb_group(0, 0, 0, "s")
+        Y(5, 0, 0, "y2")
+        Y(5, 0, 1, "y2")
+        E(5, 1)
         Y(5, 1, 1, "y2")
+        E(5, 0)
+        Y(7, 1, 0, "y1")
+        Y(7, 1, 1, "y1")
+        HT(4, 1)
+        SQ(7, 1, 0)
+        SQ(7, 1, 1)
+        HT(4, 0)
         HE(4, 1, "s")
         HE(4, 0, "s")
-        FG(5, 0, 1)
-        FG(5, 0, 0)
-        Y(7, 0, 0, "y1")
-        Y(7, 0, 1, "y1")
-        Z(1)
-        hb_quant(0, 0, 1)
-        RT(6, 0)
-        HQ(4)
-        SQ(7, 0, 0)
-        E(5, 1)
-        GATE(6)
-        RT(6, 1)
+        C(6)
+        FG(5, 1, 1)
         Y(5, 1, 0, "y2")
+        FG(5, 0, 0)
+        FG(5, 0, 1)
+        Y(7, 0, 0, "y1")
+        RT(6, 0)
+        RT(6, 1)
+        Z(1)
+        SQ(7, 0, 0)
+        FG(5, 1, 0)
+        ZE(1)
+        Y(7, 0, 1, "y1")
+        HQ(4)
         SQ(7, 0, 1)
         Y(6, 0, 0, "y2")
-        FG(5, 1, 1)
-        FG(5, 1, 0)
+        hb_quant(0, 0, 0)
         Y(6, 0, 1, "y2")
-        E(6, 0)
-        ZE(1)
-        C(7)
-        HT(5, 1)
-        HT(5, 0)
+        E(6, 1)
         Y(6, 1, 1, "y2")
+        E(6, 0)
+        HT(5, 1)
+        hb_group(0, 1, 0, "s")
+        HT(5, 0)
         HE(5, 1, "s")
         HE(5, 0, "s")
-        FG(6, 0, 1)
-        FG(6, 0, 0)
-        Z(2)
-        RT(7, 0)
-        HQ(5)
-        E(6, 1)
-        GATE(7)
-        RT(7, 1)
-        Y(6, 1, 0, "y2")
-        hb_group(0, 0, 0, "s")
-        Y(7, 0, 0, "y2")
+        C(7)
         FG(6, 1, 1)
+        Y(6, 1, 0, "y2")
+        FG(6, 0, 0)
+        FG(6, 0, 1)
+        RT(7, 0)
+        RT(7, 1)
+        hb_quant(0, 1, 0)
+        Z(2)
         FG(6, 1, 0)
+        ZE(2)
+        HQ(5)
+        hb_quant(0, 1, 1)
+        Y(7, 0, 0, "y2")
         Y(7, 0, 1, "y2")
+        E(7, 1)
+        Y(7, 1, 1, "y2")
         E(7, 0)
-        ZE(2, "v")
+        hb_group(0, 0, 1, "s")
         HT(6, 1)
         HT(6, 0)
-        Y(7, 1, 1, "y2")
         HE(6, 1, "s")
         HE(6, 0, "s")
-        FG(7, 0, 1)
-        FG(7, 0, 0)
-        hb_quant(0, 0, 0)
-        Z(3)
-        HQ(6)
-        E(7, 1)
-        Y(7, 1, 0, "y2")
         FG(7, 1, 1)
+        Y(7, 1, 0, "y2")
+        FG(7, 0, 0)
+        FG(7, 0, 1)
+        Z(3)
         FG(7, 1, 0)
-        ZE(3)
-        Z(5)
+        hb_quant(0, 0, 1)
+        ZE(3, "v")
+        HQ(6)
+        PG2()
+        Z(4)
+        HT(7, 0)
         hb_group(1, 1, 0, "s")
         hb_group(1, 0, 0, "v")
-        HT(7, 0)
-        hb_quant(1, 0, 0)
-        PG2()
         hb_quant(1, 1, 0)
-        ZE(5)
-        EM(1, 0, 0)
-        ES(1, 0, 0)
-        EM(2, 0, 0)
+        hb_quant(1, 0, 0)
         EM(2, 0, 1)
-        ES(2, 0, 0)
-        EM(1, 0, 1)
-        hb_group(1, 0, 1, "v")
-        EM(0, 0, 1)
-        Z(4)
-        EM(0, 0, 0)
-        HE(7, 0, "s")
+        hb_group(1, 0, 1, "s")
+        EM(2, 0, 0)
         hb_group(1, 1, 1, "v")
-        ES(1, 0, 1)
-        ES(2, 0, 1)
-        hb_quant(1, 0, 1)
-        ZE(4)
-        EM(0, 1, 0)
-        EA(1, 0)
-        ES(0, 0, 1)
+        EM(3, 0, 1)
         EM(3, 0, 0)
-        hb_quant(1, 1, 1)
-        EA(2, 0)
-        ES(0, 0, 0)
-        EM(0, 1, 1)
-        EM(3, 1, 0)
+        ES(2, 0, 1)
+        EM(1, 0, 0)
+        ES(2, 0, 0)
+        ES(3, 0, 1)
+        ES(3, 0, 0)
+        HE(7, 0, "s")
+        ZE(4, "v")
         HT(7, 1)
+        hb_quant(1, 0, 1)
+        EA(2, 0)
+        EA(3, 0)
+        EM(0, 0, 1)
+        EM(1, 0, 1)
+        EM(0, 0, 0)
+        HE(7, 1, "s")
+        EP(2, 0)
+        hb_quant(1, 1, 1)
+        ES(0, 0, 1)
+        Z(5)
+        ES(1, 0, 0)
+        EM(1, 1, 0)
+        ES(0, 0, 0)
+        EP(3, 0)
+        EM(1, 1, 1)
+        EM(0, 1, 0)
+        EA(0, 0)
+        ES(1, 0, 1)
+        ZE(5)
+        ES(1, 1, 0)
+        EM(0, 1, 1)
+        EM(2, 1, 1)
+        EA(1, 0)
+        EM(2, 1, 0)
+        ES(1, 1, 1)
+        EP(0, 0)
+        EM(3, 1, 0)
         ES(0, 1, 0)
         ES(0, 1, 1)
-        EM(3, 0, 1)
         EP(1, 0)
-        EA(0, 0)
-        ES(3, 0, 0)
-        Z(6)
-        EP(2, 0)
-        HE(7, 1, "s")
-        EP(0, 0)
-        ES(3, 0, 1)
-        EA(0, 1)
-        EM(3, 1, 1)
-        ES(3, 1, 0)
-        EM(1, 1, 0)
-        EM(1, 1, 1)
-        HQ(7)
-        EA(3, 0)
-        ES(3, 1, 1)
-        EP(0, 1)
-        EA(3, 1)
-        EP(3, 0)
-        EM(2, 1, 0)
-        ES(1, 1, 0)
-        ES(1, 1, 1)
-        ES(2, 1, 0)
-        EM(2, 1, 1)
-        ES(2, 1, 1)
-        EP(3, 1)
-        ZE(6)
         EA(1, 1)
+        HQ(7)
+        ES(2, 1, 1)
         Z(7)
-        ZE(7)
-        EA(2, 1)
+        EM(3, 1, 1)
+        EA(0, 1)
+        ES(2, 1, 0)
+        ES(3, 1, 0)
         EP(1, 1)
+        EA(2, 1)
+        ZE(7)
+        EP(0, 1)
+        ES(3, 1, 1)
+        Z(6)
+        EA(3, 1)
+        ZE(6)
+        EP(3, 1)
         EP(2, 1)

from contextlib import ExitStack

import concourse.mybir as mybir
from concourse.masks import make_identity

T, A, B, U, R = 1024, 512, 1024, 512, 512
FLOPS = 2 * T * A * B * 4 + 2 * T * B * U * 2 + 2 * R * T * B * 2

F32 = mybir.dt.float32
BF16 = mybir.dt.bfloat16
U32 = mybir.dt.uint32
U8 = mybir.dt.uint8
FP8 = mybir.dt.float8_e4m3fn
FP8X4 = mybir.dt.float8_e4m3fn_x4
ACT = mybir.ActivationFunctionType
ALU = mybir.AluOpType

P = 128
PACK = 4
HALF = 512
YB = {"y2": 4, "y1": 2}
TB = 2


def tile_limited_beam_combining_f6_kernel(
    tc, xr_bytes, xr_scale, xi, sr, si, window, gain, cr, ci, d, z_gain, p_gain, out_0, out_1
):
    nc = tc.nc
    with ExitStack() as ctx:
        const = ctx.enter_context(tc.tile_pool(name="const", bufs=1))
        xin = ctx.enter_context(tc.tile_pool(name="xin", bufs=2))
        rawp = ctx.enter_context(tc.tile_pool(name="rawp", bufs=3))
        grp = ctx.enter_context(tc.tile_pool(name="grp", bufs=6))
        lim = ctx.enter_context(tc.tile_pool(name="lim", bufs=2))
        keep = ctx.enter_context(tc.tile_pool(name="keep", bufs=1))
        outp = ctx.enter_context(tc.tile_pool(name="outp", bufs=2))
        psum = ctx.enter_context(tc.psum_pool(name="psum", bufs=1))
        ctx.enter_context(tc.manual_schedule())

        xr_view = xr_bytes.rearrange("(g p t) a -> g p t a", p=P, t=PACK)
        xi_view = xi.rearrange("(g p t) a -> g p t a", p=P, t=PACK)
        x_codes_in = [xin.tile([P, PACK, A], U8, name="xr_u8") for g in range(2)]
        xi_in = [xin.tile([P, PACK, A], BF16, name="xi_in") for g in range(2)]
        s_raw = [rawp.tile([P, PACK, B], BF16, name="raw") for ri in range(2)]
        s_view = [src.rearrange("(p j) w -> p j w", j=PACK) for src in (sr, si)]
        scale_rows = const.tile([P, A], F32, name="scale_rows")
        nc.gpsimd.memset(scale_rows[:], 0.0)
        ident = const.tile([P, P], F32, name="ident")
        make_identity(nc, ident[:])
        ones_f = const.tile([P, P], F32, name="ones_f")
        nc.vector.memset(ones_f[:], 1.0)
        warm = const.tile([P, 1], F32, name="warm")
        nc.vector.memset(warm[:], 1.0)
        gain_bc = const.tile([P, B], BF16, name="gain_bc")
        window_bf = const.tile([P, 2, PACK], BF16, name="window_bf")
        z_gain_bf = const.tile([P, 2, PACK], BF16, name="z_gain_bf")
        p_gain_bc = const.tile([P, B], BF16, name="p_gain_bc")
        c_raw = {}
        d_raw = {}

        def LD_scale():
            nc.scalar.dma_start(out=scale_rows[0:1, :], in_=xr_scale)
            warm_out = const.tile([P, 1], F32, name="warm_out")
            nc.scalar.activation(out=warm_out[:], in_=warm[:], func=ACT.Abs_reciprocal_sqrt)

        def LD_s(ri, h):
            cs = slice(HALF * h, HALF * (h + 1))
            nc.sync.dma_start(out=s_raw[ri][:, :, cs], in_=s_view[ri][:, :, cs])

        def LD_x(g, ri, pair):
            ts = slice(2 * pair, 2 * pair + 2)
            if ri == 0:
                nc.sync.dma_start(out=x_codes_in[g][:, ts, :], in_=xr_view[g][:, ts, :])
            else:
                nc.sync.dma_start(out=xi_in[g][:, ts, :], in_=xi_view[g][:, ts, :])

        def LD_gain():
            nc.sync.dma_start(out=gain_bc[:], in_=gain.partition_broadcast(P))

        def LD_cols():
            nc.sync.dma_start(out=window_bf[:], in_=window.rearrange("(g p t) -> p g t", p=P, t=PACK))
            nc.sync.dma_start(out=z_gain_bf[:], in_=z_gain.rearrange("(g p t) -> p g t", p=P, t=PACK))

        def LD_c(k):
            c_raw[k] = rawp.tile([P, 2, PACK, U], BF16, name="raw")
            nc.sync.dma_start(out=c_raw[k][:], in_=(cr, ci)[k].rearrange("(g p j) v -> p g j v", p=P, j=PACK))

        def LD_d():
            d_raw[0] = rawp.tile([P, 4, T], BF16, name="raw")
            nc.sync.dma_start(out=d_raw[0][:], in_=d.rearrange("(q p) i -> p q i", p=P))

        def LD_pg():
            nc.sync.dma_start(out=p_gain_bc[:], in_=p_gain.partition_broadcast(P))

        window_cols = const.tile([P, 2, PACK], F32, name="window_cols")
        z_gain_cols = const.tile([P, 2, PACK], F32, name="z_gain_cols")
        scale_bc = const.tile([P, A], F32, name="scale_bc")
        pg2_bc = const.tile([P, B], F32, name="pg2_bc")

        def broadcast(lhsT, row, out, func):
            bank = psum.tile([P, HALF], F32, name="bank", tag="tr", bufs=TB)
            nc.tensor.matmul(bank[:], lhsT=lhsT, rhs=row, start=True, stop=True)
            nc.scalar.activation(out=out, in_=bank[:], func=func)

        x_q = {}
        xrb = {}
        gx = {}

        def x_product(g, ts):
            if g not in xrb:
                xrb[g] = xin.tile([P, PACK, A], BF16, name="xrb")
            for t in ts:
                nc.vector.tensor_tensor(
                    out=xrb[g][:, t, :], in0=x_codes_in[g][:, t, :].bitcast(FP8), in1=scale_bc[:], op=ALU.mult
                )

        xb = {}

        def XT(g, ri, pair):
            src = (xrb, xi_in)[ri][g]
            bank = psum.tile([P, 4, P], F32, name="bank", tag="tr", bufs=TB)
            for tt in range(2):
                words = src[:, 2 * pair + tt, :].bitcast(F32)
                for u in range(2):
                    nc.tensor.transpose(bank[:, 2 * tt + u, :], words[:, u : A // 2 : 2], ident[:])
            xb[(g, ri, pair)] = bank

        def XE(g, ri, pair, engine="s"):
            if (g, ri) not in gx:
                gx[(g, ri)] = grp.tile([P, 2048], BF16, name="grouped", align_bytes=64)
            copy = nc.vector.tensor_copy if engine == "v" else nc.scalar.copy
            copy(
                out=gx[(g, ri)][:, 1024 * pair : 1024 * (pair + 1)].bitcast(F32).rearrange("p (k i u) -> p k i u", k=2, u=2),
                in_=xb[(g, ri, pair)][:].rearrange("p (k u) i -> p k i u", u=2),
            )

        def x_quant(g, ri):
            codes = keep.tile([P, 512], U32, name="xq%d%d" % (g, ri), align_bytes=64)
            scales = keep.tile([P, 512], U8, name="xs%d%d" % (g, ri), align_bytes=64)
            nc.vector.quantize_mx(out=codes[:].bitcast(FP8X4), scales=scales[:], in_=gx[(g, ri)][:])
            for t in range(PACK):
                cs = slice(128 * t, 128 * t + 128)
                x_q[(g, t, ri)] = (codes[:, cs].bitcast(FP8X4), scales[:, cs])

        def interleave(engine, dst, src):
            o = dst.rearrange("p (c i t) -> p c t i", i=4, t=PACK)
            s = src.rearrange("p t (c i) -> p c t i", i=4)
            if engine == "v":
                nc.vector.tensor_copy(out=o, in_=s)
            else:
                nc.scalar.copy(out=o, in_=s)

        s_codes = [keep.tile([P, B], U32, name="s_codes%d" % k, align_bytes=64) for k in range(3)]
        s_scales = [keep.tile([P, B], U8, name="s_scales%d" % k, align_bytes=64) for k in range(3)]
        sg = {}

        def s_group(ri, h, engine):
            sg[(ri, h)] = grp.tile([P, 2048], BF16, name="grouped", align_bytes=64)
            dst = sg[(ri, h)][:].rearrange("p (u q e t) -> p u q t e", u=2, e=2, t=PACK)
            src = s_raw[ri][:, :, HALF * h : HALF * (h + 1)].rearrange("p t (q u e) -> p u q t e", u=2, e=2)
            copy = nc.vector.tensor_copy if engine == "v" else nc.scalar.copy
            for u in range(2):
                copy(out=dst[:, u], in_=src[:, u])

        def s_neg(h):
            sg[(2, h)] = grp.tile([P, 2048], BF16, name="grouped", align_bytes=64)
            nc.vector.tensor_scalar(out=sg[(2, h)][:], in0=sg[(1, h)][:], scalar1=-1.0, scalar2=None, op0=ALU.mult)

        def s_quant(k, h):
            cs = slice(HALF * h, HALF * (h + 1))
            nc.vector.quantize_mx(out=s_codes[k][:, cs].bitcast(FP8X4), scales=s_scales[k][:, cs], in_=sg[(k, h)][:])

        def s_op(k, h):
            cs = slice(HALF * h, HALF * (h + 1))
            return s_codes[k][:, cs].bitcast(FP8X4), s_scales[k][:, cs]

        def mx(out, lhs, rhs, start, stop):
            nc.tensor.matmul_mx(
                out=out, lhsT=lhs[0], lhsT_scale=lhs[1], rhs=rhs[0], rhs_scale=rhs[1], start=start, stop=stop
            )

        h_bf = [[keep.tile([P, PACK, B], BF16, name="h%d%d" % (g, ri)) for ri in range(2)] for g in range(2)]
        y = {}
        sq = {}
        level = {}
        power = {}

        def Y(n, h, ri, tag):
            g, t = divmod(n, PACK)
            bank = psum.tile([P, HALF], F32, name="y", tag=tag, bufs=YB[tag])
            mx(bank[:], x_q[(g, t, ri)], s_op(0, h), True, False)
            mx(bank[:], x_q[(g, t, 1 - ri)], s_op(1 + ri, h), False, True)
            y[(n, ri, h, tag)] = bank

        def SQ(n, h, ri):
            if n not in sq:
                sq[n] = lim.tile([P, 2, B], F32, name="sq")
            cs = slice(HALF * h, HALF * (h + 1))
            nc.scalar.activation(out=sq[n][:, ri, cs], in_=y[(n, ri, h, "y1")][:], func=ACT.Square, scale=1.0 / 32.0)

        def C(n):
            level[n] = lim.tile([P, 1], F32, name="level", bufs=3)
            power[n] = lim.tile([P, B], F32, name="power", bufs=3)
            nc.vector.scalar_tensor_tensor(
                out=power[n][:], in0=sq[n][:, 0, :], scalar=1.0, in1=sq[n][:, 1, :], op0=ALU.mult, op1=ALU.add, accum_out=level[n][:]
            )

        def RT(n, h):
            cs = slice(HALF * h, HALF * (h + 1))
            nc.scalar.activation(
                out=power[n][:, cs], in_=power[n][:, cs], func=ACT.Abs_reciprocal_sqrt, scale=1024.0, bias=level[n][:]
            )

        def E(n, h):
            g, t = divmod(n, PACK)
            cs = slice(HALF * h, HALF * (h + 1))
            nc.vector.scalar_tensor_tensor(
                out=power[n][:, cs], in0=power[n][:, cs], scalar=window_cols[:, g, t : t + 1], in1=gain_perm[:, cs], op0=ALU.mult, op1=ALU.mult
            )

        def FG(n, h, ri):
            g, t = divmod(n, PACK)
            cs = slice(HALF * h, HALF * (h + 1))
            nc.vector.tensor_tensor(out=h_bf[g][ri][:, t, cs], in0=y[(n, ri, h, "y2")][:], in1=power[n][:, cs], op=ALU.mult)

        c_codes = [keep.tile([P, 2 * U], U32, name="c_codes%d" % k, align_bytes=64) for k in range(2)]
        c_scales = [keep.tile([P, 2 * U], U8, name="c_scales%d" % k, align_bytes=64) for k in range(2)]
        cg = {}

        def c_group(k, gg, part, engine):
            if (k, gg) not in cg:
                cg[(k, gg)] = grp.tile([P, 2048], BF16, name="grouped", align_bytes=64)
            o = cg[(k, gg)][:, 1024 * part : 1024 * (part + 1)].rearrange("p (c i t) -> p c t i", i=4, t=PACK)
            s = c_raw[k][:, gg, :, 256 * part : 256 * (part + 1)].rearrange("p t (c i) -> p c t i", i=4)
            if engine == "s":
                nc.scalar.activation(out=o, in_=s, func=ACT.Copy, scale=(1.0, -1.0)[k])
            else:
                nc.vector.tensor_scalar(out=o, in0=s, scalar1=(1.0, -1.0)[k], scalar2=None, op0=ALU.mult)

        def c_quant(k, gg):
            cs = slice(U * gg, U * (gg + 1))
            nc.vector.quantize_mx(out=c_codes[k][:, cs].bitcast(FP8X4), scales=c_scales[k][:, cs], in_=cg[(k, gg)][:])

        d_codes = [keep.tile([P, R], U32, name="d_codes%d" % g, align_bytes=64) for g in range(2)]
        d_scales = [keep.tile([P, R], U8, name="d_scales%d" % g, align_bytes=64) for g in range(2)]
        dg = {}

        db = {}

        def DT(g, qq):
            bank = psum.tile([P, 4, P], F32, name="bank", tag="tr", bufs=TB)
            for k in range(2):
                words = d_raw[0][:, 2 * qq + k, :].bitcast(F32)
                for u in range(2):
                    nc.tensor.transpose(bank[:, 2 * k + u, :], words[:, 256 * g + u : 256 * (g + 1) : 2], ident[:])
            db[(g, qq)] = bank

        def DE(g, qq, engine="s"):
            if g not in dg:
                dg[g] = grp.tile([P, 2048], BF16, name="grouped", align_bytes=64)
            copy = nc.vector.tensor_copy if engine == "v" else nc.scalar.copy
            copy(
                out=dg[g][:, 1024 * qq : 1024 * (qq + 1)].bitcast(F32).rearrange("p (k i u) -> p k i u", k=2, u=2),
                in_=db[(g, qq)][:].rearrange("p (k u) i -> p k i u", u=2),
            )

        def d_quant(g):
            nc.vector.quantize_mx(out=d_codes[g][:].bitcast(FP8X4), scales=d_scales[g][:], in_=dg[g][:])

        z_view = out_0.rearrange("(g p t) v -> g p t v", p=P, t=PACK)
        hg_t = {}
        ht = {}
        zbank = {}

        htb = {}

        def HT(n, ri):
            g, t = divmod(n, PACK)
            bank = psum.tile([P, 4, P], F32, name="bank", tag="tr", bufs=TB)
            words = h_bf[g][ri][:, t, :].bitcast(F32)
            for gg in range(2):
                for u in range(2):
                    nc.tensor.transpose(bank[:, 2 * gg + u, :], words[:, 256 * gg + 128 * u : 256 * gg + 128 * (u + 1)], ident[:])
            htb[(n, ri)] = bank

        def HE(n, ri, engine="s"):
            if n not in hg_t:
                hg_t[n] = grp.tile([P, 2048], BF16, name="grouped", align_bytes=64)
            copy = nc.vector.tensor_copy if engine == "v" else nc.scalar.copy
            copy(
                out=hg_t[n][:, 1024 * ri : 1024 * (ri + 1)].bitcast(F32).rearrange("p (k i u) -> p k i u", k=2, u=2),
                in_=htb[(n, ri)][:].rearrange("p (k u) i -> p k i u", u=2),
            )

        def HQ(n):
            codes = lim.tile([P, 512], U32, name="ht_codes", align_bytes=64, bufs=4)
            scales = lim.tile([P, 512], U8, name="ht_scales", align_bytes=64, bufs=4)
            nc.vector.quantize_mx(out=codes[:].bitcast(FP8X4), scales=scales[:], in_=hg_t[n][:])
            ht[n] = (codes, scales)

        def Z(n):
            codes, scales = ht[n]
            z = psum.tile([P, U], F32, name="z", tag="tr", bufs=TB)
            for k in range(4):
                ri, gg = divmod(k, 2)
                cs = slice(256 * ri + 128 * gg, 256 * ri + 128 * gg + 128)
                vs = slice(U * gg, U * (gg + 1))
                mx(
                    z[:],
                    (codes[:, cs].bitcast(FP8X4), scales[:, cs]),
                    (c_codes[ri][:, vs].bitcast(FP8X4), c_scales[ri][:, vs]),
                    k == 0,
                    k == 3,
                )
            zbank[n] = z

        def PG2():
            nc.scalar.activation(out=pg2_bc[:], in_=p_gain_bc[:], func=ACT.Square)

        gain_perm = const.tile([P, B], BF16, name="gain_perm")

        def COLS():
            for h in range(2):
                cs = slice(HALF * h, HALF * (h + 1))
                nc.vector.tensor_copy(
                    out=gain_perm[:, cs].rearrange("p (u q e) -> p u q e", u=2, e=2),
                    in_=gain_bc[:, cs].rearrange("p (q u e) -> p u q e", u=2, e=2),
                )
            nc.vector.tensor_copy(out=window_cols[:], in_=window_bf[:])
            nc.vector.tensor_copy(out=z_gain_cols[:], in_=z_gain_bf[:])

        def BC():
            broadcast(ones_f[:], scale_rows[:], scale_bc[:], ACT.Copy)

        def ZE(n, engine="s"):
            g, t = divmod(n, PACK)
            z_sb = outp.tile([P, U], F32, name="z_sb")
            if engine == "s":
                nc.scalar.activation(out=z_sb[:], in_=zbank[n][:], func=ACT.Copy, scale=z_gain_cols[:, g, t : t + 1])
            else:
                nc.vector.tensor_scalar(out=z_sb[:], in0=zbank[n][:], scalar1=z_gain_cols[:, g, t : t + 1], scalar2=None, op0=ALU.mult)
            nc.sync.dma_start(out=z_view[g][:, t, :], in_=z_sb[:])

        hb_codes = [[keep.tile([P, B], U32, name="hb_codes%d%d" % (g, ri), align_bytes=64) for ri in range(2)] for g in range(2)]
        hb_scales = [[keep.tile([P, B], U8, name="hb_scales%d%d" % (g, ri), align_bytes=64) for ri in range(2)] for g in range(2)]
        hbg = {}

        def hb_group(g, ri, h, engine, part=None):
            if (g, ri, h) not in hbg:
                hbg[(g, ri, h)] = grp.tile([P, 2048], BF16, name="grouped", align_bytes=64)
            lo, hi = (0, HALF) if part is None else (256 * part, 256 * (part + 1))
            src = h_bf[g][ri][:, :, HALF * h + lo : HALF * h + hi]
            dst = hbg[(g, ri, h)][:, PACK * lo : PACK * hi]
            interleave(engine, dst, src)

        def hb_quant(g, ri, h):
            cs = slice(HALF * h, HALF * (h + 1))
            nc.vector.quantize_mx(
                out=hb_codes[g][ri][:, cs].bitcast(FP8X4), scales=hb_scales[g][ri][:, cs], in_=hbg[(g, ri, h)][:]
            )

        esq = {}

        ebank = {}

        def EM(q, h, ri):
            cs = slice(HALF * h, HALF * (h + 1))
            rs = slice(P * q, P * (q + 1))
            e = psum.tile([P, HALF], F32, name="y", tag="y2", bufs=YB["y2"])
            for g in range(2):
                mx(
                    e[:],
                    (d_codes[g][:, rs].bitcast(FP8X4), d_scales[g][:, rs]),
                    (hb_codes[g][ri][:, cs].bitcast(FP8X4), hb_scales[g][ri][:, cs]),
                    g == 0,
                    g == 1,
                )
            ebank[(q, h, ri)] = e

        def ES(q, h, ri):
            if (q, h) not in esq:
                esq[(q, h)] = lim.tile([P, 2, HALF], F32, name="sq")
            nc.scalar.activation(out=esq[(q, h)][:, ri, :], in_=ebank[(q, h, ri)][:], func=ACT.Square)

        total = {}

        def EA(q, h):
            total[(q, h)] = outp.tile([P, HALF], F32, name="total")
            nc.vector.tensor_tensor(out=total[(q, h)][:], in0=esq[(q, h)][:, 0, :], in1=esq[(q, h)][:, 1, :], op=ALU.add)

        def EP(q, h):
            cs = slice(HALF * h, HALF * (h + 1))
            o = outp.tile([P, HALF], F32, name="o_map", bufs=4)
            nc.vector.tensor_tensor(
                out=o[:].rearrange("p (q u e) -> p q u e", u=2, e=2),
                in0=total[(q, h)][:].rearrange("p (u q e) -> p q u e", u=2, e=2),
                in1=pg2_bc[:, cs].rearrange("p (q u e) -> p q u e", u=2, e=2),
                op=ALU.mult,
            )
            nc.sync.dma_start(out=out_1[P * q : P * (q + 1), cs], in_=o[:])

        LD_scale()
        LD_s(1, 0)
        LD_x(0, 0, 1)
        s_group(1, 0, "v")
        s_quant(1, 0)
        LD_x(0, 1, 1)
        LD_x(0, 1, 0)
        LD_s(0, 0)
        LD_x(0, 0, 0)
        BC()
        x_product(0, (3,))
        s_neg(0)
        XT(0, 1, 1)
        XE(0, 1, 1)
        x_product(0, (0,))
        x_product(0, (1,))
        XT(0, 1, 0)
        LD_s(1, 1)
        x_product(0, (2,))
        XE(0, 1, 0)
        LD_s(0, 1)
        x_quant(0, 1)
        s_group(0, 0, "s")
        XT(0, 0, 0)
        XT(0, 0, 1)
        XE(0, 0, 0)
        LD_cols()
        LD_x(1, 0, 1)
        s_quant(0, 0)
        s_quant(2, 0)
        XE(0, 0, 1)
        x_quant(0, 0)
        s_group(0, 1, "v")
        Y(0, 0, 1, "y1")
        s_group(1, 1, "s")
        LD_c(1)
        Y(0, 0, 0, "y2")
        SQ(0, 0, 1)
        LD_pg()
        Y(1, 0, 0, "y1")
        Y(0, 0, 1, "y2")
        s_neg(1)
        s_quant(0, 1)
        Y(0, 0, 0, "y1")
        SQ(1, 0, 0)
        s_quant(2, 1)
        SQ(0, 0, 0)
        s_quant(1, 1)
        Y(0, 1, 1, "y1")
        LD_x(1, 0, 0)
        LD_x(1, 1, 0)
        SQ(0, 1, 1)
        x_product(1, (2,))
        x_product(1, (0,))
        Y(0, 1, 0, "y1")
        Y(1, 1, 1, "y1")
        SQ(0, 1, 0)
        C(0)
        SQ(1, 1, 1)
        Y(1, 1, 0, "y1")
        SQ(1, 1, 0)
        RT(0, 0)
        LD_gain()
        LD_x(1, 1, 1)
        LD_c(0)
        Y(1, 0, 1, "y1")
        x_product(1, (1,))
        COLS()
        SQ(1, 0, 1)
        x_product(1, (3,))
        RT(0, 1)
        LD_d()
        E(0, 1)
        Y(0, 1, 1, "y2")
        E(0, 0)
        Y(2, 1, 0, "y1")
        Y(2, 1, 1, "y1")
        XT(1, 1, 0)
        SQ(2, 1, 0)
        SQ(2, 1, 1)
        XT(1, 1, 1)
        XE(1, 1, 0)
        C(1)
        FG(0, 1, 1)
        XT(1, 0, 0)
        Y(0, 1, 0, "y2")
        c_group(1, 1, 0, "v")
        FG(0, 0, 0)
        c_group(1, 0, 1, "s")
        FG(0, 0, 1)
        Y(2, 0, 0, "y1")
        RT(1, 0)
        RT(1, 1)
        SQ(2, 0, 0)
        FG(0, 1, 0)
        Y(2, 0, 1, "y1")
        XE(1, 1, 1)
        SQ(2, 0, 1)
        Y(1, 0, 0, "y2")
        Y(1, 0, 1, "y2")
        XE(1, 0, 0, "v")
        E(1, 1)
        Y(1, 1, 1, "y2")
        E(1, 0)
        Y(3, 1, 0, "y1")
        Y(3, 1, 1, "y1")
        c_group(1, 0, 0, "s")
        HT(0, 1)
        SQ(3, 1, 0)
        SQ(3, 1, 1)
        HT(0, 0)
        HE(0, 1, "s")
        HE(0, 0, "s")
        C(2)
        FG(1, 1, 1)
        Y(1, 1, 0, "y2")
        FG(1, 0, 0)
        c_group(1, 1, 1, "v")
        DT(1, 1)
        FG(1, 0, 1)
        XT(1, 0, 1)
        x_quant(1, 1)
        Y(3, 0, 0, "y1")
        RT(2, 0)
        RT(2, 1)
        XE(1, 0, 1)
        SQ(3, 0, 0)
        FG(1, 1, 0)
        DE(1, 1)
        x_quant(1, 0)
        Y(3, 0, 1, "y1")
        HQ(0)
        c_quant(1, 1)
        SQ(3, 0, 1)
        Y(2, 0, 0, "y2")
        Y(2, 0, 1, "y2")
        E(2, 1)
        Y(2, 1, 1, "y2")
        E(2, 0)
        Y(4, 1, 0, "y1")
        c_group(0, 0, 0, "s")
        Y(4, 1, 1, "y1")
        c_group(0, 0, 1, "s")
        HT(1, 1)
        SQ(4, 1, 0)
        SQ(4, 1, 1)
        HT(1, 0)
        HE(1, 1, "s")
        c_quant(1, 0)
        HE(1, 0, "s")
        C(3)
        FG(2, 1, 1)
        Y(2, 1, 0, "y2")
        FG(2, 0, 0)
        FG(2, 0, 1)
        Y(4, 0, 0, "y1")
        DT(1, 0)
        RT(3, 0)
        RT(3, 1)
        SQ(4, 0, 0)
        FG(2, 1, 0)
        Y(4, 0, 1, "y1")
        HQ(1)
        SQ(4, 0, 1)
        Y(3, 0, 0, "y2")
        c_group(0, 1, 1, "s")
        Y(3, 0, 1, "y2")
        DE(1, 0)
        E(3, 1)
        Y(3, 1, 1, "y2")
        E(3, 0)
        Y(5, 1, 0, "y1")
        c_quant(0, 0)
        Y(5, 1, 1, "y1")
        HT(2, 1)
        SQ(5, 1, 0)
        SQ(5, 1, 1)
        HT(2, 0)
        HE(2, 1, "s")
        HE(2, 0, "s")
        C(4)
        FG(3, 1, 1)
        Y(3, 1, 0, "y2")
        FG(3, 0, 0)
        FG(3, 0, 1)
        Y(5, 0, 0, "y1")
        RT(4, 0)
        RT(4, 1)
        SQ(5, 0, 0)
        FG(3, 1, 0)
        Y(5, 0, 1, "y1")
        HQ(2)
        SQ(5, 0, 1)
        Y(4, 0, 0, "y2")
        DT(0, 0)
        DT(0, 1)
        Y(4, 0, 1, "y2")
        d_quant(1)
        E(4, 1)
        Y(4, 1, 1, "y2")
        c_group(0, 1, 0, "s")
        DE(0, 0)
        E(4, 0)
        Y(6, 1, 0, "y1")
        DE(0, 1)
        Y(6, 1, 1, "y1")
        HT(3, 1)
        SQ(6, 1, 0)
        SQ(6, 1, 1)
        HT(3, 0)
        c_quant(0, 1)
        HE(3, 1, "s")
        HE(3, 0, "s")
        C(5)
        hb_group(0, 1, 1, "v")
        FG(4, 1, 1)
        Y(4, 1, 0, "y2")
        FG(4, 0, 0)
        FG(4, 0, 1)
        Y(6, 0, 0, "y1")
        RT(5, 0)
        RT(5, 1)
        Z(0)
        SQ(6, 0, 0)
        FG(4, 1, 0)
        ZE(0)
        Y(6, 0, 1, "y1")
        HQ(3)
        d_quant(0)
        SQ(6, 0, 1)
        hb_group(0, 0, 0, "s")
        Y(5, 0, 0, "y2")
        Y(5, 0, 1, "y2")
        E(5, 1)
        Y(5, 1, 1, "y2")
        E(5, 0)
        Y(7, 1, 0, "y1")
        Y(7, 1, 1, "y1")
        HT(4, 1)
        SQ(7, 1, 0)
        SQ(7, 1, 1)
        HT(4, 0)
        HE(4, 1, "s")
        HE(4, 0, "s")
        C(6)
        FG(5, 1, 1)
        Y(5, 1, 0, "y2")
        FG(5, 0, 0)
        FG(5, 0, 1)
        Y(7, 0, 0, "y1")
        RT(6, 0)
        RT(6, 1)
        Z(1)
        SQ(7, 0, 0)
        FG(5, 1, 0)
        ZE(1)
        Y(7, 0, 1, "y1")
        HQ(4)
        SQ(7, 0, 1)
        Y(6, 0, 0, "y2")
        hb_quant(0, 0, 0)
        Y(6, 0, 1, "y2")
        E(6, 1)
        Y(6, 1, 1, "y2")
        E(6, 0)
        HT(5, 1)
        hb_group(0, 1, 0, "s")
        HT(5, 0)
        HE(5, 1, "s")
        HE(5, 0, "s")
        C(7)
        FG(6, 1, 1)
        Y(6, 1, 0, "y2")
        FG(6, 0, 0)
        FG(6, 0, 1)
        RT(7, 0)
        RT(7, 1)
        hb_quant(0, 1, 0)
        Z(2)
        FG(6, 1, 0)
        ZE(2)
        HQ(5)
        hb_quant(0, 1, 1)
        Y(7, 0, 0, "y2")
        Y(7, 0, 1, "y2")
        E(7, 1)
        Y(7, 1, 1, "y2")
        E(7, 0)
        hb_group(0, 0, 1, "s")
        HT(6, 1)
        HT(6, 0)
        HE(6, 1, "s")
        HE(6, 0, "s")
        FG(7, 1, 1)
        Y(7, 1, 0, "y2")
        FG(7, 0, 0)
        FG(7, 0, 1)
        Z(3)
        FG(7, 1, 0)
        hb_quant(0, 0, 1)
        ZE(3, "v")
        HQ(6)
        PG2()
        Z(4)
        HT(7, 0)
        hb_group(1, 1, 0, "s")
        hb_group(1, 0, 0, "v")
        hb_quant(1, 1, 0)
        hb_quant(1, 0, 0)
        EM(2, 0, 1)
        hb_group(1, 0, 1, "s")
        EM(2, 0, 0)
        hb_group(1, 1, 1, "v")
        EM(3, 0, 1)
        EM(3, 0, 0)
        ES(2, 0, 1)
        EM(1, 0, 0)
        ES(2, 0, 0)
        ES(3, 0, 1)
        ES(3, 0, 0)
        HE(7, 0, "s")
        ZE(4, "v")
        HT(7, 1)
        hb_quant(1, 0, 1)
        EA(2, 0)
        EA(3, 0)
        EM(0, 0, 1)
        EM(1, 0, 1)
        EM(0, 0, 0)
        HE(7, 1, "s")
        EP(2, 0)
        hb_quant(1, 1, 1)
        ES(0, 0, 1)
        Z(5)
        ES(1, 0, 0)
        EM(1, 1, 0)
        ES(0, 0, 0)
        EP(3, 0)
        EM(1, 1, 1)
        EM(0, 1, 0)
        EA(0, 0)
        ES(1, 0, 1)
        ZE(5)
        ES(1, 1, 0)
        EM(0, 1, 1)
        EM(2, 1, 1)
        EA(1, 0)
        EM(2, 1, 0)
        ES(1, 1, 1)
        EP(0, 0)
        EM(3, 1, 0)
        ES(0, 1, 0)
        ES(0, 1, 1)
        EP(1, 0)
        EA(1, 1)
        HQ(7)
        ES(2, 1, 1)
        Z(7)
        EM(3, 1, 1)
        EA(0, 1)
        ES(2, 1, 0)
        ES(3, 1, 0)
        EP(1, 1)
        EA(2, 1)
        ZE(7)
        EP(0, 1)
        ES(3, 1, 1)
        Z(6)
        EA(3, 1)
        ZE(6)
        EP(3, 1)
        EP(2, 1)
